import numpy as np
import ml_dtypes


def mxq(x, axis, fmt="e4m3"):
    dtype, down = {"e4m3": (ml_dtypes.float8_e4m3fn, 7), "e5m2": (ml_dtypes.float8_e5m2, 14)}[fmt]
    v = np.moveaxis(np.asarray(x, np.float32).astype(ml_dtypes.bfloat16).astype(np.float64), axis, -1)
    blocks = v.reshape(v.shape[:-1] + (-1, 32))
    amax = np.abs(blocks).max(-1, keepdims=True)
    byte = np.maximum(np.where(amax > 0, np.frexp(amax)[1] - 1 + 127, 0) - down, 1)
    scale = np.exp2(byte - 127.0)
    codes = (blocks / scale).astype(np.float32).astype(dtype).astype(np.float64)
    return np.moveaxis((codes * scale).reshape(v.shape), -1, axis)


WIDE = False


def mx_kscale(k):
    if not WIDE:
        return np.ones(k)
    levels = np.array([10, -10, 5, -5, 0])
    if k % 512:
        return np.exp2(np.random.permutation(np.resize(levels, k // 32))).repeat(32)
    a = np.empty((k // 512, 16))
    for p in range(k // 512):
        a[p, :8] = np.random.permutation(np.resize(levels, 8))
        for g in range(8):
            far = levels[np.abs(levels - a[p, g]) >= 10]
            a[p, g + 8] = far[np.random.randint(len(far))]
    return np.exp2(a.ravel()).repeat(32)


def f64(x):
    return np.asarray(x).astype(np.float64)


def striped(idx):
    return np.tile(idx.reshape(-1, 16).T, (8, 1)).astype(np.uint16)


def unstriped(offs):
    return offs[:16].T.reshape(-1).astype(np.int64)


K, T, E, C, N = 1024, 1024, 16, 128, 256


def by_expert(wq, xq):
    return np.concatenate([wq[e].T @ xq[:, e * C:(e + 1) * C] for e in range(E)], axis=1)


def setup_inputs():
    n = np.random.standard_normal
    s = mx_kscale(K)[:, None]
    first = np.random.permutation(np.repeat(np.arange(E), T // E))
    second = (first + 1 + np.random.permutation(np.repeat(np.arange(E - 1), -(-T // (E - 1)))[:T])) % E
    while np.bincount(second, minlength=E).max() != T // E:
        load = np.bincount(second, minlength=E); hi, lo = int(load.argmax()), int(load.argmin())
        t = np.flatnonzero((second == hi) & (first != lo))[0]; second[t] = lo
    slot_token = np.empty(E * C, np.int64); pos = np.empty((2, T), np.int64); fill = np.zeros(E, np.int64)
    place = np.stack([np.random.permutation(C) for _ in range(E)])
    for r, deal in enumerate((first, second)):
        for t in np.random.permutation(T):
            e = deal[t]; j = e * C + place[e, fill[e]]; fill[e] += 1; slot_token[j] = t; pos[r, t] = j
    g = np.random.uniform(0.2, 0.8, T)
    return {
        "xT": (n((K, T)) * s).astype(np.float32),
        "w": (n((E, K, N)) / np.sqrt(K) / s[None]).astype(np.float32),
        "gate": np.stack([np.tile(g, (N, 1)), np.tile(1.0 - g, (N, 1))]).astype(np.float32),
        "offs": striped(slot_token),
        "pos1": striped(pos[0]),
        "pos2": striped(pos[1]),
    }


def reference(xT, w, gate, offs, pos1, pos2):
    idx = unstriped(offs)
    xq = mxq(f64(xT)[:, idx], 0, "e4m3")
    y = by_expert(mxq(f64(w), 1, "e4m3"), xq)
    return f64(gate[0]) * y[:, unstriped(pos1)] + f64(gate[1]) * y[:, unstriped(pos2)]

@@ -1,0 +1,189 @@
+from contextlib import ExitStack
+
+import concourse.mybir as mybir
+
+K, T, E, C, N = 1024, 1024, 16, 128, 256
+FLOPS = 2 * K * N * E * C
+
+F32 = mybir.dt.float32
+BF16 = mybir.dt.bfloat16
+U32 = mybir.dt.uint32
+U16 = mybir.dt.uint16
+U8 = mybir.dt.uint8
+FP8X4 = mybir.dt.float8_e4m3fn_x4
+MULT = mybir.AluOpType.mult
+ADD = mybir.AluOpType.add
+
+P = 128
+CH = 512
+RAW_BUFS = 7
+FAST = True
+LOADS = ["x00", "x01", "w0", "x02", "w1", "x03", "x10", "x11", "x12", "x13"] + ["w%d" % e for e in range(2, 16)] + ["g0", "g1"]
+UNITS = [(0, 0), (1, 0), (0, 1), (1, 1), (2, 0), (2, 1), (3, 0), (3, 1)]
+V_HALVES = [(5, 1), (7, 1), (9, 1), (11, 1), (13, 1), (14, 1), (15, 0), (15, 1)]
+TOK = 512
+
+
+def tile_routed_moe_kernel(tc, xT, w, gate, offs, pos1, pos2, out):
+    nc = tc.nc
+    with ExitStack() as ctx:
+        lists = ctx.enter_context(tc.tile_pool(name="lists", bufs=1))
+        raw = ctx.enter_context(tc.tile_pool(name="raw", bufs=RAW_BUFS))
+        keep = ctx.enter_context(tc.tile_pool(name="keep", bufs=1))
+        stage = ctx.enter_context(tc.tile_pool(name="stage", bufs=3))
+        wq = ctx.enter_context(tc.tile_pool(name="wq", bufs=4))
+        fin = ctx.enter_context(tc.tile_pool(name="fin", bufs=3))
+        psum = ctx.enter_context(tc.psum_pool(name="psum", bufs=3))
+
+        offs_sb = lists.tile([P, E * C // 16], U16, name="offs_sb")
+        nc.sync.dma_start(offs_sb[:], offs)
+        xv = xT.rearrange("(g p t) n -> g p t n", p=P, t=4)
+        gv = gate.rearrange("r (h p) t -> h p r t", p=P)
+        xp, wr, gt = {}, {}, {}
+        for what in LOADS:
+            if what[0] == "x":
+                g, t = int(what[1]), int(what[2])
+                xp[g, t] = keep.tile([P, T], F32, name="xp%d%d" % (g, t))
+                nc.sync.dma_start(out=xp[g, t][:], in_=xv[g, :, t, :])
+            elif what[0] == "w":
+                e = int(what[1:])
+                wr[e] = raw.tile([P, 2 * 4 * N], F32, name="wr%d" % e, tag="raw")
+                nc.sync.dma_start(
+                    out=wr[e][:].rearrange("p (g f) -> p g f", g=2),
+                    in_=w[e].rearrange("(g p j) n -> p g (j n)", g=2, p=P, j=4),
+                )
+            else:
+                h = int(what[1])
+                gt[h] = raw.tile([P, 2 * T], F32, name="gt%d" % h, tag="raw")
+                nc.sync.dma_start(out=gt[h][:].rearrange("p (r t) -> p r t", r=2), in_=gv[h])
+        pos_sb = []
+        for r, lst in enumerate((pos1, pos2)):
+            pos_sb.append(lists.tile([P, T // 16], U16, name="pos_sb%d" % r))
+            nc.sync.dma_start(pos_sb[r][:], lst)
+
+        g4, tb, tcod, tscl, wb, wcod, wscl, acc = {}, {}, {}, {}, {}, {}, {}, {}
+        y = [keep.tile([P, E * C], F32, name="y%d" % h) for h in range(2)]
+
+        def interleave(copy, dst, src):
+            if FAST:
+                copy(out=dst.rearrange("p (c i) j -> p c j i", i=4), in_=src.rearrange("p j (c i) -> p c j i", i=4))
+            else:
+                copy(out=dst, in_=src.rearrange("p j n -> p n j"))
+
+        def gather(c, g, t):
+            if t == 0:
+                g4[c, g] = stage.tile([P, 4, CH], F32, name="g4", tag="g4")
+            nc.vector.tensor_copy(g4[c, g][:, t, :], xp[g, t][:].indirect(offs_sb[:, c * (CH // 16) : (c + 1) * (CH // 16)]))
+
+        def interleave_tokens(c, g):
+            if c not in tb:
+                tb[c] = stage.tile([P, 2 * CH * 4], BF16, name="tb", tag="tb", bufs=2, align_bytes=64)
+            interleave(nc.scalar.copy, tb[c][:].rearrange("p (g n t) -> p g n t", g=2, t=4)[:, g], g4[c, g][:])
+
+        def quantize_tokens(c):
+            tcod[c] = keep.tile([P, 2 * CH], U32, name="tcod%d" % c, align_bytes=64)
+            tscl[c] = keep.tile([P, 2 * CH], U8, name="tscl%d" % c, align_bytes=64)
+            nc.vector.quantize_mx(out=tcod[c][:].bitcast(FP8X4), scales=tscl[c][:], in_=tb[c][:])
+
+        def interleave_weights(e, g):
+            if e // 2 not in wb:
+                wb[e // 2] = stage.tile([P, 2 * 2 * N * 4], BF16, name="wb", tag="wb", bufs=3, align_bytes=64)
+            src = wr[e][:].rearrange("p (g j n) -> p g j n", g=2, j=4)
+            dst = wb[e // 2][:].rearrange("p (e g n j) -> p e g n j", e=2, g=2, j=4)
+            interleave(nc.vector.tensor_copy if (e, g) in V_HALVES else nc.scalar.copy, dst[:, e % 2, g], src[:, g])
+
+        def quantize_weights(pair):
+            wcod[pair] = wq.tile([P, 4 * N], U32, name="wcod", tag="wcod", align_bytes=64)
+            wscl[pair] = wq.tile([P, 4 * N], U8, name="wscl", tag="wscl", align_bytes=64)
+            nc.vector.quantize_mx(out=wcod[pair][:].bitcast(FP8X4), scales=wscl[pair][:], in_=wb[pair][:])
+
+        def multiply(pair):
+            for h in range(2):
+                acc[h] = psum.tile([P, 2 * C], F32, name="acc%d" % h, tag="acc%d" % h)
+                for i in range(2):
+                    e = 2 * pair + i
+                    c, s0 = e // (CH // C), (e % (CH // C)) * C
+                    for g in range(2):
+                        wcols = slice((2 * i + g) * N + h * P, (2 * i + g) * N + (h + 1) * P)
+                        tcols = slice(g * CH + s0, g * CH + s0 + C)
+                        nc.tensor.matmul_mx(
+                            out=acc[h][:, i * C : (i + 1) * C],
+                            lhsT=wcod[pair][:, wcols].bitcast(FP8X4),
+                            lhsT_scale=wscl[pair][:, wcols],
+                            rhs=tcod[c][:, tcols].bitcast(FP8X4),
+                            rhs_scale=tscl[c][:, tcols],
+                            start=(g == 0),
+                            stop=(g == 1),
+                        )
+                nc.scalar.copy(out=y[h][:, 2 * pair * C : 2 * (pair + 1) * C], in_=acc[h][:])
+
+        waiting = []
+
+        def multiply_ready():
+            for pair in list(waiting):
+                if pair // 2 in tcod:
+                    multiply(pair)
+                    waiting.remove(pair)
+
+        for t in range(4):
+            gather(0, 0, t)
+            gather(1, 0, t)
+            if t >= 2:
+                interleave_weights(t - 2, 0)
+                interleave_weights(t - 2, 1)
+        for r in range(2, len(UNITS) + 2):
+            unit = UNITS[r] if r < len(UNITS) else None
+            done = [UNITS[0], UNITS[1]] if r == 2 else [UNITS[r - 1]] if r <= len(UNITS) else []
+            pair = r - 1
+            if done:
+                interleave_tokens(*done[0])
+            if unit:
+                gather(unit[0], unit[1], 0)
+            if pair - 1 < E // 2:
+                quantize_weights(pair - 1)
+                waiting.append(pair - 1)
+            if pair < E // 2:
+                interleave_weights(2 * pair, 0)
+                interleave_weights(2 * pair, 1)
+            if unit:
+                gather(unit[0], unit[1], 1)
+            if len(done) == 2:
+                interleave_tokens(*done[1])
+            if unit:
+                gather(unit[0], unit[1], 2)
+            if done and done[0][1] == 1:
+                quantize_tokens(done[0][0])
+            multiply_ready()
+            if pair < E // 2:
+                interleave_weights(2 * pair + 1, 0)
+                interleave_weights(2 * pair + 1, 1)
+            if unit:
+                gather(unit[0], unit[1], 3)
+        multiply_ready()
+        assert not waiting
+
+        steps = [(h, t0) for h in range(2) for t0 in range(0, T, TOK)]
+        parts = {}
+
+        def fetch(s):
+            h, t0 = steps[s]
+            for r in range(2):
+                parts[s, r] = fin.tile([P, TOK], F32, name="part%d" % r, tag="part%d" % r)
+                nc.vector.tensor_tensor(
+                    parts[s, r][:],
+                    y[h][:].indirect(pos_sb[r][:, t0 // 16 : (t0 + TOK) // 16]),
+                    gt[h][:, r * T + t0 : r * T + t0 + TOK],
+                    MULT,
+                )
+
+        def finish(s):
+            h, t0 = steps[s]
+            o = fin.tile([P, TOK], F32, name="o", tag="o")
+            nc.vector.tensor_tensor(o[:], parts[s, 0][:], parts[s, 1][:], ADD)
+            nc.sync.dma_start(out=out[h * P : (h + 1) * P, t0 : t0 + TOK], in_=o[:])
+
+        fetch(0)
+        for s in range(1, len(steps)):
+            fetch(s)
+            finish(s - 1)
+        finish(len(steps) - 1)

@@ -15,12 +15,12 @@ MULT = mybir.AluOpType.mult
 ADD = mybir.AluOpType.add
 
 P = 128
-CH = 512
-RAW_BUFS = 7
-FAST = True
-LOADS = ["x00", "x01", "w0", "x02", "w1", "x03", "x10", "x11", "x12", "x13"] + ["w%d" % e for e in range(2, 16)] + ["g0", "g1"]
-UNITS = [(0, 0), (1, 0), (0, 1), (1, 1), (2, 0), (2, 1), (3, 0), (3, 1)]
-V_HALVES = [(5, 1), (7, 1), (9, 1), (11, 1), (13, 1), (14, 1), (15, 0), (15, 1)]
+PAIRS = E // 2
+RAW_BUFS = 6
+WB_BUFS = 3
+LOADS = ["x00", "x01", "w0", "x02", "w1", "x03", "w2", "x10", "w3", "x11", "w4", "x12", "w5", "x13"] + ["w%d" % e for e in range(6, 16)] + ["g0", "g1"]
+FIRST = 4
+V_EXPERTS = []
 TOK = 512
 
 
@@ -30,21 +30,20 @@ def tile_routed_moe_kernel(tc, xT, w, gate, offs, pos1, pos2, out):
         lists = ctx.enter_context(tc.tile_pool(name="lists", bufs=1))
         raw = ctx.enter_context(tc.tile_pool(name="raw", bufs=RAW_BUFS))
         keep = ctx.enter_context(tc.tile_pool(name="keep", bufs=1))
-        stage = ctx.enter_context(tc.tile_pool(name="stage", bufs=3))
-        wq = ctx.enter_context(tc.tile_pool(name="wq", bufs=4))
-        fin = ctx.enter_context(tc.tile_pool(name="fin", bufs=3))
-        psum = ctx.enter_context(tc.psum_pool(name="psum", bufs=3))
+        stage = ctx.enter_context(tc.tile_pool(name="stage", bufs=WB_BUFS))
+        fin = ctx.enter_context(tc.tile_pool(name="fin", bufs=2))
+        psum = ctx.enter_context(tc.psum_pool(name="psum", bufs=1))
 
         offs_sb = lists.tile([P, E * C // 16], U16, name="offs_sb")
         nc.sync.dma_start(offs_sb[:], offs)
         xv = xT.rearrange("(g p t) n -> g p t n", p=P, t=4)
         gv = gate.rearrange("r (h p) t -> h p r t", p=P)
-        xp, wr, gt = {}, {}, {}
+        xq = [keep.tile([P, 4, T], F32, name="xq%d" % g) for g in range(2)]
+        wr, gt = {}, {}
         for what in LOADS:
             if what[0] == "x":
                 g, t = int(what[1]), int(what[2])
-                xp[g, t] = keep.tile([P, T], F32, name="xp%d%d" % (g, t))
-                nc.sync.dma_start(out=xp[g, t][:], in_=xv[g, :, t, :])
+                nc.sync.dma_start(out=xq[g][:, t, :], in_=xv[g, :, t, :])
             elif what[0] == "w":
                 e = int(what[1:])
                 wr[e] = raw.tile([P, 2 * 4 * N], F32, name="wr%d" % e, tag="raw")
@@ -61,106 +60,62 @@ def tile_routed_moe_kernel(tc, xT, w, gate, offs, pos1, pos2, out):
             pos_sb.append(lists.tile([P, T // 16], U16, name="pos_sb%d" % r))
             nc.sync.dma_start(pos_sb[r][:], lst)
 
-        g4, tb, tcod, tscl, wb, wcod, wscl, acc = {}, {}, {}, {}, {}, {}, {}, {}
         y = [keep.tile([P, E * C], F32, name="y%d" % h) for h in range(2)]
+        acc = [[psum.tile([P, 4 * C], F32, name="acc%d_%d" % (h, q)) for q in range(E // 4)] for h in range(2)]
+        tb = [keep.tile([P, 2 * 2 * C * 4], BF16, name="tb%d" % pr, align_bytes=64) for pr in range(PAIRS)]
+        tcod = [keep.tile([P, 2 * 2 * C], U32, name="tcod%d" % pr, align_bytes=64) for pr in range(PAIRS)]
+        tscl = [keep.tile([P, 2 * 2 * C], U8, name="tscl%d" % pr, align_bytes=64) for pr in range(PAIRS)]
+        wcod = [keep.tile([P, 4 * N], U32, name="wcod%d" % pr, align_bytes=64) for pr in range(PAIRS)]
+        wscl = [keep.tile([P, 4 * N], U8, name="wscl%d" % pr, align_bytes=64) for pr in range(PAIRS)]
 
-        def interleave(copy, dst, src):
-            if FAST:
-                copy(out=dst.rearrange("p (c i) j -> p c j i", i=4), in_=src.rearrange("p j (c i) -> p c j i", i=4))
-            else:
-                copy(out=dst, in_=src.rearrange("p j n -> p n j"))
+        for pr in range(PAIRS):
+            wb = stage.tile([P, 2 * 2 * N * 4], BF16, name="wb", tag="wb", align_bytes=64)
+            dst = wb[:].rearrange("p (e g n j) -> p e g n j", e=2, g=2, j=4)
+            for i in range(2):
+                e = 2 * pr + i
+                src = wr[e][:].rearrange("p (g j n) -> p g j n", g=2, j=4)
+                copy = nc.vector.tensor_copy if e in V_EXPERTS else nc.scalar.copy
+                copy(out=dst[:, i], in_=src.rearrange("p g j n -> p g n j"))
+            nc.vector.quantize_mx(out=wcod[pr][:].bitcast(FP8X4), scales=wscl[pr][:], in_=wb[:])
 
-        def gather(c, g, t):
-            if t == 0:
-                g4[c, g] = stage.tile([P, 4, CH], F32, name="g4", tag="g4")
-            nc.vector.tensor_copy(g4[c, g][:, t, :], xp[g, t][:].indirect(offs_sb[:, c * (CH // 16) : (c + 1) * (CH // 16)]))
+        def gather(e, g, t):
+            dst = tb[e // 2][:].rearrange("p (e g n t) -> p e g n t", e=2, g=2, t=4)
+            nc.vector.tensor_copy(dst[:, e % 2, g, :, t], xq[g][:, t, :].indirect(offs_sb[:, e * (C // 16) : (e + 1) * (C // 16)]))
 
-        def interleave_tokens(c, g):
-            if c not in tb:
-                tb[c] = stage.tile([P, 2 * CH * 4], BF16, name="tb", tag="tb", bufs=2, align_bytes=64)
-            interleave(nc.scalar.copy, tb[c][:].rearrange("p (g n t) -> p g n t", g=2, t=4)[:, g], g4[c, g][:])
-
-        def quantize_tokens(c):
-            tcod[c] = keep.tile([P, 2 * CH], U32, name="tcod%d" % c, align_bytes=64)
-            tscl[c] = keep.tile([P, 2 * CH], U8, name="tscl%d" % c, align_bytes=64)
-            nc.vector.quantize_mx(out=tcod[c][:].bitcast(FP8X4), scales=tscl[c][:], in_=tb[c][:])
-
-        def interleave_weights(e, g):
-            if e // 2 not in wb:
-                wb[e // 2] = stage.tile([P, 2 * 2 * N * 4], BF16, name="wb", tag="wb", bufs=3, align_bytes=64)
-            src = wr[e][:].rearrange("p (g j n) -> p g j n", g=2, j=4)
-            dst = wb[e // 2][:].rearrange("p (e g n j) -> p e g n j", e=2, g=2, j=4)
-            interleave(nc.vector.tensor_copy if (e, g) in V_HALVES else nc.scalar.copy, dst[:, e % 2, g], src[:, g])
-
-        def quantize_weights(pair):
-            wcod[pair] = wq.tile([P, 4 * N], U32, name="wcod", tag="wcod", align_bytes=64)
-            wscl[pair] = wq.tile([P, 4 * N], U8, name="wscl", tag="wscl", align_bytes=64)
-            nc.vector.quantize_mx(out=wcod[pair][:].bitcast(FP8X4), scales=wscl[pair][:], in_=wb[pair][:])
-
-        def multiply(pair):
+        def finish_pair(pr):
+            nc.vector.quantize_mx(out=tcod[pr][:].bitcast(FP8X4), scales=tscl[pr][:], in_=tb[pr][:])
             for h in range(2):
-                acc[h] = psum.tile([P, 2 * C], F32, name="acc%d" % h, tag="acc%d" % h)
                 for i in range(2):
-                    e = 2 * pair + i
-                    c, s0 = e // (CH // C), (e % (CH // C)) * C
+                    e = 2 * pr + i
                     for g in range(2):
                         wcols = slice((2 * i + g) * N + h * P, (2 * i + g) * N + (h + 1) * P)
-                        tcols = slice(g * CH + s0, g * CH + s0 + C)
+                        tcols = slice((2 * i + g) * C, (2 * i + g + 1) * C)
                         nc.tensor.matmul_mx(
-                            out=acc[h][:, i * C : (i + 1) * C],
-                            lhsT=wcod[pair][:, wcols].bitcast(FP8X4),
-                            lhsT_scale=wscl[pair][:, wcols],
-                            rhs=tcod[c][:, tcols].bitcast(FP8X4),
-                            rhs_scale=tscl[c][:, tcols],
+                            out=acc[h][e // 4][:, (e % 4) * C : (e % 4 + 1) * C],
+                            lhsT=wcod[pr][:, wcols].bitcast(FP8X4),
+                            lhsT_scale=wscl[pr][:, wcols],
+                            rhs=tcod[pr][:, tcols].bitcast(FP8X4),
+                            rhs_scale=tscl[pr][:, tcols],
                             start=(g == 0),
                             stop=(g == 1),
                         )
-                nc.scalar.copy(out=y[h][:, 2 * pair * C : 2 * (pair + 1) * C], in_=acc[h][:])
+                first = pr - 1 if pr % 2 == 1 and pr < PAIRS - 1 else pr
+                if pr % 2 == 1 or pr == PAIRS - 2:
+                    copy = nc.vector.tensor_copy if (pr == PAIRS - 1 and h == 0) else nc.scalar.copy
+                    copy(out=y[h][:, first * 2 * C : (pr + 1) * 2 * C], in_=acc[h][pr // 2][:, (first % 2) * 2 * C : (pr % 2 + 1) * 2 * C])
 
-        waiting = []
-
-        def multiply_ready():
-            for pair in list(waiting):
-                if pair // 2 in tcod:
-                    multiply(pair)
-                    waiting.remove(pair)
-
-        for t in range(4):
-            gather(0, 0, t)
-            gather(1, 0, t)
-            if t >= 2:
-                interleave_weights(t - 2, 0)
-                interleave_weights(t - 2, 1)
-        for r in range(2, len(UNITS) + 2):
-            unit = UNITS[r] if r < len(UNITS) else None
-            done = [UNITS[0], UNITS[1]] if r == 2 else [UNITS[r - 1]] if r <= len(UNITS) else []
-            pair = r - 1
-            if done:
-                interleave_tokens(*done[0])
-            if unit:
-                gather(unit[0], unit[1], 0)
-            if pair - 1 < E // 2:
-                quantize_weights(pair - 1)
-                waiting.append(pair - 1)
-            if pair < E // 2:
-                interleave_weights(2 * pair, 0)
-                interleave_weights(2 * pair, 1)
-            if unit:
-                gather(unit[0], unit[1], 1)
-            if len(done) == 2:
-                interleave_tokens(*done[1])
-            if unit:
-                gather(unit[0], unit[1], 2)
-            if done and done[0][1] == 1:
-                quantize_tokens(done[0][0])
-            multiply_ready()
-            if pair < E // 2:
-                interleave_weights(2 * pair + 1, 0)
-                interleave_weights(2 * pair + 1, 1)
-            if unit:
-                gather(unit[0], unit[1], 3)
-        multiply_ready()
-        assert not waiting
+        for g in range(2):
+            for t in range(4):
+                for e in range(2 * FIRST):
+                    gather(e, g, t)
+        for pr in range(FIRST):
+            finish_pair(pr)
+        for pr in range(FIRST, PAIRS):
+            for g in range(2):
+                for t in range(4):
+                    for i in range(2):
+                        gather(2 * pr + i, g, t)
+            finish_pair(pr)
 
         steps = [(h, t0) for h in range(2) for t0 in range(0, T, TOK)]
         parts = {}

@@ -15,13 +15,18 @@ MULT = mybir.AluOpType.mult
 ADD = mybir.AluOpType.add
 
 P = 128
+CH = 512
 PAIRS = E // 2
-RAW_BUFS = 6
+RAW_BUFS = 3
+G4_BUFS = 3
 WB_BUFS = 3
-LOADS = ["x00", "x01", "w0", "x02", "w1", "x03", "w2", "x10", "w3", "x11", "w4", "x12", "w5", "x13"] + ["w%d" % e for e in range(6, 16)] + ["g0", "g1"]
-FIRST = 4
-V_EXPERTS = []
-TOK = 512
+LOADS = ["x00", "x01", "w0", "x02", "x03", "w1", "x10", "x11", "x12", "x13"] + ["w%d" % pr for pr in range(2, 8)] + ["g"]
+UNITS = [(0, 0), (1, 0), (0, 1), (1, 1), (2, 0), (2, 1), (3, 0), (3, 1)]
+WSPLIT = [0, 0, 256, 0, 256, 256, 256, 512]
+TSPLIT = [0, 0, 0, 256, 0, 0, 0, 256]
+TOKS = [[1024], [768, 256]]
+WPIECES = [2, 1, 1, 1, 1, 1, 1, 1]
+WQ_BUFS = 4
 
 
 def tile_routed_moe_kernel(tc, xT, w, gate, offs, pos1, pos2, out):
@@ -30,31 +35,31 @@ def tile_routed_moe_kernel(tc, xT, w, gate, offs, pos1, pos2, out):
         lists = ctx.enter_context(tc.tile_pool(name="lists", bufs=1))
         raw = ctx.enter_context(tc.tile_pool(name="raw", bufs=RAW_BUFS))
         keep = ctx.enter_context(tc.tile_pool(name="keep", bufs=1))
-        stage = ctx.enter_context(tc.tile_pool(name="stage", bufs=WB_BUFS))
+        stage = ctx.enter_context(tc.tile_pool(name="stage", bufs=2))
         fin = ctx.enter_context(tc.tile_pool(name="fin", bufs=2))
         psum = ctx.enter_context(tc.psum_pool(name="psum", bufs=1))
 
         offs_sb = lists.tile([P, E * C // 16], U16, name="offs_sb")
         nc.sync.dma_start(offs_sb[:], offs)
         xv = xT.rearrange("(g p t) n -> g p t n", p=P, t=4)
+        wv = w.rearrange("e (g p j) n -> e g p j n", g=2, p=P, j=4)
         gv = gate.rearrange("r (h p) t -> h p r t", p=P)
-        xq = [keep.tile([P, 4, T], F32, name="xq%d" % g) for g in range(2)]
-        wr, gt = {}, {}
+        xp, wr = {}, {}
         for what in LOADS:
             if what[0] == "x":
                 g, t = int(what[1]), int(what[2])
-                nc.sync.dma_start(out=xq[g][:, t, :], in_=xv[g, :, t, :])
+                xp[g, t] = keep.tile([P, T], F32, name="xp%d%d" % (g, t))
+                nc.sync.dma_start(out=xp[g, t][:], in_=xv[g, :, t, :])
             elif what[0] == "w":
-                e = int(what[1:])
-                wr[e] = raw.tile([P, 2 * 4 * N], F32, name="wr%d" % e, tag="raw")
-                nc.sync.dma_start(
-                    out=wr[e][:].rearrange("p (g f) -> p g f", g=2),
-                    in_=w[e].rearrange("(g p j) n -> p g (j n)", g=2, p=P, j=4),
-                )
+                pr = int(what[1:])
+                wr[pr] = raw.tile([P, 4, 4 * N], F32, name="wr%d" % pr, tag="raw")
+                for i in range(2):
+                    for g in range(2):
+                        nc.sync.dma_start(out=wr[pr][:, :, (2 * i + g) * N : (2 * i + g + 1) * N], in_=wv[2 * pr + i, g])
             else:
-                h = int(what[1])
-                gt[h] = raw.tile([P, 2 * T], F32, name="gt%d" % h, tag="raw")
-                nc.sync.dma_start(out=gt[h][:].rearrange("p (r t) -> p r t", r=2), in_=gv[h])
+                gt = raw.tile([P, 2, 2, T], F32, name="gt", tag="raw")
+                for h in range(2):
+                    nc.sync.dma_start(out=gt[:, h], in_=gv[h])
         pos_sb = []
         for r, lst in enumerate((pos1, pos2)):
             pos_sb.append(lists.tile([P, T // 16], U16, name="pos_sb%d" % r))
@@ -62,80 +67,131 @@ def tile_routed_moe_kernel(tc, xT, w, gate, offs, pos1, pos2, out):
 
         y = [keep.tile([P, E * C], F32, name="y%d" % h) for h in range(2)]
         acc = [[psum.tile([P, 4 * C], F32, name="acc%d_%d" % (h, q)) for q in range(E // 4)] for h in range(2)]
-        tb = [keep.tile([P, 2 * 2 * C * 4], BF16, name="tb%d" % pr, align_bytes=64) for pr in range(PAIRS)]
-        tcod = [keep.tile([P, 2 * 2 * C], U32, name="tcod%d" % pr, align_bytes=64) for pr in range(PAIRS)]
-        tscl = [keep.tile([P, 2 * 2 * C], U8, name="tscl%d" % pr, align_bytes=64) for pr in range(PAIRS)]
-        wcod = [keep.tile([P, 4 * N], U32, name="wcod%d" % pr, align_bytes=64) for pr in range(PAIRS)]
-        wscl = [keep.tile([P, 4 * N], U8, name="wscl%d" % pr, align_bytes=64) for pr in range(PAIRS)]
+        last = {}
+        tcod = [keep.tile([P, 2 * CH], U32, name="tcod%d" % c, align_bytes=64) for c in range(4)]
+        tscl = [keep.tile([P, 2 * CH], U8, name="tscl%d" % c, align_bytes=64) for c in range(4)]
+        g4, tb, wb, wcod, wscl = {}, {}, {}, {}, {}
 
-        for pr in range(PAIRS):
-            wb = stage.tile([P, 2 * 2 * N * 4], BF16, name="wb", tag="wb", align_bytes=64)
-            dst = wb[:].rearrange("p (e g n j) -> p e g n j", e=2, g=2, j=4)
-            for i in range(2):
-                e = 2 * pr + i
-                src = wr[e][:].rearrange("p (g j n) -> p g j n", g=2, j=4)
-                copy = nc.vector.tensor_copy if e in V_EXPERTS else nc.scalar.copy
-                copy(out=dst[:, i], in_=src.rearrange("p g j n -> p g n j"))
-            nc.vector.quantize_mx(out=wcod[pr][:].bitcast(FP8X4), scales=wscl[pr][:], in_=wb[:])
+        def interleave(dst, src, n, n_vector, pieces=1):
+            n_scalar = n - n_vector
+            shares = [(nc.scalar.copy, k * n_scalar // pieces, (k + 1) * n_scalar // pieces) for k in range(pieces)]
+            for copy, lo, hi in shares + [(nc.vector.tensor_copy, n_scalar, n)]:
+                if hi > lo:
+                    copy(
+                        out=dst[:, lo:hi, :].rearrange("p (c i) j -> p c j i", i=4),
+                        in_=src[:, :, lo:hi].rearrange("p j (c i) -> p c j i", i=4),
+                    )
 
-        def gather(e, g, t):
-            dst = tb[e // 2][:].rearrange("p (e g n t) -> p e g n t", e=2, g=2, t=4)
-            nc.vector.tensor_copy(dst[:, e % 2, g, :, t], xq[g][:, t, :].indirect(offs_sb[:, e * (C // 16) : (e + 1) * (C // 16)]))
+        def gather(u, t):
+            c, g = UNITS[u]
+            if t == 0:
+                g4[u] = stage.tile([P, 4, CH], F32, name="g4", tag="g4", bufs=G4_BUFS)
+            nc.vector.tensor_copy(g4[u][:, t, :], xp[g, t][:].indirect(offs_sb[:, c * (CH // 16) : (c + 1) * (CH // 16)]))
 
-        def finish_pair(pr):
-            nc.vector.quantize_mx(out=tcod[pr][:].bitcast(FP8X4), scales=tscl[pr][:], in_=tb[pr][:])
+        def interleave_tokens(u):
+            c, g = UNITS[u]
+            if c not in tb:
+                tb[c] = stage.tile([P, 2, CH, 4], BF16, name="tb", tag="tb", align_bytes=64)
+            interleave(tb[c][:, g], g4[u][:], CH, TSPLIT[u])
+
+        def quantize_tokens(c):
+            nc.vector.quantize_mx(out=tcod[c][:].bitcast(FP8X4), scales=tscl[c][:], in_=tb[c][:].rearrange("p g n t -> p (g n t)"))
+
+        def interleave_weights(pr):
+            wb[pr] = stage.tile([P, 4 * N, 4], BF16, name="wb", tag="wb", bufs=WB_BUFS, align_bytes=64)
+            interleave(wb[pr][:], wr[pr][:], 4 * N, WSPLIT[pr], WPIECES[pr])
+
+        def quantize_weights(pr):
+            wcod[pr] = stage.tile([P, 4 * N], U32, name="wcod", tag="wcod", bufs=WQ_BUFS, align_bytes=64)
+            wscl[pr] = stage.tile([P, 4 * N], U8, name="wscl", tag="wscl", bufs=WQ_BUFS, align_bytes=64)
+            nc.vector.quantize_mx(out=wcod[pr][:].bitcast(FP8X4), scales=wscl[pr][:], in_=wb[pr][:].rearrange("p m j -> p (m j)"))
+
+        def multiply(pr):
             for h in range(2):
+                if pr == PAIRS - 1:
+                    if h == 1:
+                        nc.scalar.copy(out=y[1][:, 0 : 4 * C], in_=acc[1][0][:])
+                    last[h] = psum.tile([P, 2 * C], F32, name="last%d" % h, tag="acc%d_0" % h)
                 for i in range(2):
                     e = 2 * pr + i
+                    c, s0 = e // 4, (e % 4) * C
                     for g in range(2):
                         wcols = slice((2 * i + g) * N + h * P, (2 * i + g) * N + (h + 1) * P)
-                        tcols = slice((2 * i + g) * C, (2 * i + g + 1) * C)
+                        tcols = slice(g * CH + s0, g * CH + s0 + C)
                         nc.tensor.matmul_mx(
-                            out=acc[h][e // 4][:, (e % 4) * C : (e % 4 + 1) * C],
+                            out=last[h][:, i * C : (i + 1) * C] if pr == PAIRS - 1 else acc[h][c][:, s0 : s0 + C],
                             lhsT=wcod[pr][:, wcols].bitcast(FP8X4),
                             lhsT_scale=wscl[pr][:, wcols],
-                            rhs=tcod[pr][:, tcols].bitcast(FP8X4),
-                            rhs_scale=tscl[pr][:, tcols],
+                            rhs=tcod[c][:, tcols].bitcast(FP8X4),
+                            rhs_scale=tscl[c][:, tcols],
                             start=(g == 0),
                             stop=(g == 1),
                         )
                 first = pr - 1 if pr % 2 == 1 and pr < PAIRS - 1 else pr
-                if pr % 2 == 1 or pr == PAIRS - 2:
-                    copy = nc.vector.tensor_copy if (pr == PAIRS - 1 and h == 0) else nc.scalar.copy
-                    copy(out=y[h][:, first * 2 * C : (pr + 1) * 2 * C], in_=acc[h][pr // 2][:, (first % 2) * 2 * C : (pr % 2 + 1) * 2 * C])
+                if h == 0 and (pr % 2 == 1 or pr == PAIRS - 2):
+                    copy = nc.vector.tensor_copy if pr == PAIRS - 1 else nc.scalar.copy
+                    src = last[h][:] if pr == PAIRS - 1 else acc[h][pr // 2][:, (first % 2) * 2 * C : (pr % 2 + 1) * 2 * C]
+                    copy(out=y[h][:, first * 2 * C : (pr + 1) * 2 * C], in_=src)
 
-        for g in range(2):
-            for t in range(4):
-                for e in range(2 * FIRST):
-                    gather(e, g, t)
-        for pr in range(FIRST):
-            finish_pair(pr)
-        for pr in range(FIRST, PAIRS):
-            for g in range(2):
+        waiting = []
+        quantized = []
+
+        def multiply_ready():
+            for pr in list(waiting):
+                if pr // 2 in quantized:
+                    multiply(pr)
+                    waiting.remove(pr)
+
+        for t in range(4):
+            gather(0, t)
+            gather(1, t)
+        interleave_weights(0)
+        for r in range(2, len(UNITS) + 2):
+            for u in [0, 1] if r == 2 else [r - 1] if r <= len(UNITS) else []:
+                interleave_tokens(u)
+                if UNITS[u][1] == 1:
+                    quantize_tokens(UNITS[u][0])
+                    quantized.append(UNITS[u][0])
+            if r - 2 < PAIRS:
+                quantize_weights(r - 2)
+                waiting.append(r - 2)
+            multiply_ready()
+            if r - 1 < PAIRS:
+                interleave_weights(r - 1)
+            if r < len(UNITS):
                 for t in range(4):
-                    for i in range(2):
-                        gather(2 * pr + i, g, t)
-            finish_pair(pr)
+                    gather(r, t)
+        multiply_ready()
+        assert not waiting
+        for q in range(1, E // 4 - 1):
+            nc.scalar.copy(out=y[1][:, q * 4 * C : (q + 1) * 4 * C], in_=acc[1][q][:])
+        nc.scalar.copy(out=y[1][:, 12 * C : 14 * C], in_=acc[1][3][:, 0 : 2 * C])
+        nc.scalar.copy(out=y[1][:, 14 * C : 16 * C], in_=last[1][:])
 
-        steps = [(h, t0) for h in range(2) for t0 in range(0, T, TOK)]
+        steps = []
+        for h in range(2):
+            t0 = 0
+            for n in TOKS[h]:
+                steps.append((h, t0, n))
+                t0 += n
         parts = {}
 
         def fetch(s):
-            h, t0 = steps[s]
+            h, t0, n = steps[s]
             for r in range(2):
-                parts[s, r] = fin.tile([P, TOK], F32, name="part%d" % r, tag="part%d" % r)
+                parts[s, r] = fin.tile([P, n], F32, name="part%d" % r, tag="part%d" % r)
                 nc.vector.tensor_tensor(
                     parts[s, r][:],
-                    y[h][:].indirect(pos_sb[r][:, t0 // 16 : (t0 + TOK) // 16]),
-                    gt[h][:, r * T + t0 : r * T + t0 + TOK],
+                    y[h][:].indirect(pos_sb[r][:] if n == T else pos_sb[r][:, t0 // 16 : (t0 + n) // 16]),
+                    gt[:, h, r, t0 : t0 + n],
                     MULT,
                 )
 
         def finish(s):
-            h, t0 = steps[s]
-            o = fin.tile([P, TOK], F32, name="o", tag="o")
+            h, t0, n = steps[s]
+            o = fin.tile([P, n], F32, name="o", tag="o", bufs=3)
             nc.vector.tensor_tensor(o[:], parts[s, 0][:], parts[s, 1][:], ADD)
-            nc.sync.dma_start(out=out[h * P : (h + 1) * P, t0 : t0 + TOK], in_=o[:])
+            nc.sync.dma_start(out=out[h * P : (h + 1) * P, t0 : t0 + n], in_=o[:])
 
         fetch(0)
         for s in range(1, len(steps)):

@@ -20,13 +20,15 @@ PAIRS = E // 2
 RAW_BUFS = 3
 G4_BUFS = 3
 WB_BUFS = 3
-LOADS = ["x00", "x01", "w0", "x02", "x03", "w1", "x10", "x11", "x12", "x13"] + ["w%d" % pr for pr in range(2, 8)] + ["g"]
+LOADS = ["x00", "x01", "x02", "w0a", "x03", "w0b", "x10", "x11", "x12", "x13"] + ["w%d" % pr for pr in range(1, 8)] + ["g"]
 UNITS = [(0, 0), (1, 0), (0, 1), (1, 1), (2, 0), (2, 1), (3, 0), (3, 1)]
-WSPLIT = [0, 0, 256, 0, 256, 256, 256, 512]
-TSPLIT = [0, 0, 0, 256, 0, 0, 0, 256]
+WSPLIT = [0, 0, 0, 0, 0, 0, 0, 256]
+TSPLIT = [0, 0, 0, 0, 0, 0, 0, 256]
 TOKS = [[1024], [768, 256]]
 WPIECES = [2, 1, 1, 1, 1, 1, 1, 1]
 WQ_BUFS = 4
+PC_LAG = 6
+HSPLIT = [6, 7]
 
 
 def tile_routed_moe_kernel(tc, xT, w, gate, offs, pos1, pos2, out):
@@ -51,11 +53,17 @@ def tile_routed_moe_kernel(tc, xT, w, gate, offs, pos1, pos2, out):
                 xp[g, t] = keep.tile([P, T], F32, name="xp%d%d" % (g, t))
                 nc.sync.dma_start(out=xp[g, t][:], in_=xv[g, :, t, :])
             elif what[0] == "w":
-                pr = int(what[1:])
-                wr[pr] = raw.tile([P, 4, 4 * N], F32, name="wr%d" % pr, tag="raw")
-                for i in range(2):
+                pr = int(what[1])
+                if pr not in wr:
+                    wr[pr] = raw.tile([P, 4, 4 * N], F32, name="wr%d" % pr, tag="raw")
+                for i in [0] if what[2:] == "a" else [1] if what[2:] == "b" else [0, 1]:
                     for g in range(2):
-                        nc.sync.dma_start(out=wr[pr][:, :, (2 * i + g) * N : (2 * i + g + 1) * N], in_=wv[2 * pr + i, g])
+                        if pr in HSPLIT:
+                            for h in range(2):
+                                m0 = ((2 * h + i) * 2 + g) * P
+                                nc.sync.dma_start(out=wr[pr][:, :, m0 : m0 + P], in_=wv[2 * pr + i, g][:, :, h * P : (h + 1) * P])
+                        else:
+                            nc.sync.dma_start(out=wr[pr][:, :, (2 * i + g) * N : (2 * i + g + 1) * N], in_=wv[2 * pr + i, g])
             else:
                 gt = raw.tile([P, 2, 2, T], F32, name="gt", tag="raw")
                 for h in range(2):
@@ -97,26 +105,36 @@ def tile_routed_moe_kernel(tc, xT, w, gate, offs, pos1, pos2, out):
         def quantize_tokens(c):
             nc.vector.quantize_mx(out=tcod[c][:].bitcast(FP8X4), scales=tscl[c][:], in_=tb[c][:].rearrange("p g n t -> p (g n t)"))
 
-        def interleave_weights(pr):
-            wb[pr] = stage.tile([P, 4 * N, 4], BF16, name="wb", tag="wb", bufs=WB_BUFS, align_bytes=64)
-            interleave(wb[pr][:], wr[pr][:], 4 * N, WSPLIT[pr], WPIECES[pr])
+        def interleave_weights(pr, half=0):
+            if half == 0:
+                wb[pr] = stage.tile([P, 4 * N, 4], BF16, name="wb", tag="wb", bufs=WB_BUFS, align_bytes=64)
+            if pr in HSPLIT:
+                cols = slice(half * 2 * N, (half + 1) * 2 * N)
+                interleave(wb[pr][:, cols, :], wr[pr][:, :, cols], 2 * N, WSPLIT[pr] if half == 0 else 0)
+            else:
+                interleave(wb[pr][:], wr[pr][:], 4 * N, WSPLIT[pr], WPIECES[pr])
 
-        def quantize_weights(pr):
-            wcod[pr] = stage.tile([P, 4 * N], U32, name="wcod", tag="wcod", bufs=WQ_BUFS, align_bytes=64)
-            wscl[pr] = stage.tile([P, 4 * N], U8, name="wscl", tag="wscl", bufs=WQ_BUFS, align_bytes=64)
-            nc.vector.quantize_mx(out=wcod[pr][:].bitcast(FP8X4), scales=wscl[pr][:], in_=wb[pr][:].rearrange("p m j -> p (m j)"))
+        def quantize_weights(pr, half=0):
+            if half == 0:
+                wcod[pr] = stage.tile([P, 4 * N], U32, name="wcod", tag="wcod", bufs=WQ_BUFS, align_bytes=64)
+                wscl[pr] = stage.tile([P, 4 * N], U8, name="wscl", tag="wscl", bufs=WQ_BUFS, align_bytes=64)
+            cols = slice(half * 2 * N, (half + 1) * 2 * N) if pr in HSPLIT else slice(0, 4 * N)
+            nc.vector.quantize_mx(
+                out=wcod[pr][:, cols].bitcast(FP8X4), scales=wscl[pr][:, cols], in_=wb[pr][:, cols, :].rearrange("p m j -> p (m j)")
+            )
 
-        def multiply(pr):
-            for h in range(2):
+        def multiply(pr, halves=(0, 1)):
+            for h in halves:
                 if pr == PAIRS - 1:
                     if h == 1:
-                        nc.scalar.copy(out=y[1][:, 0 : 4 * C], in_=acc[1][0][:])
+                        empty(1, 0)
                     last[h] = psum.tile([P, 2 * C], F32, name="last%d" % h, tag="acc%d_0" % h)
                 for i in range(2):
                     e = 2 * pr + i
                     c, s0 = e // 4, (e % 4) * C
                     for g in range(2):
-                        wcols = slice((2 * i + g) * N + h * P, (2 * i + g) * N + (h + 1) * P)
+                        w0 = ((2 * h + i) * 2 + g) * P if pr in HSPLIT else (2 * i + g) * N + h * P
+                        wcols = slice(w0, w0 + P)
                         tcols = slice(g * CH + s0, g * CH + s0 + C)
                         nc.tensor.matmul_mx(
                             out=last[h][:, i * C : (i + 1) * C] if pr == PAIRS - 1 else acc[h][c][:, s0 : s0 + C],
@@ -127,11 +145,10 @@ def tile_routed_moe_kernel(tc, xT, w, gate, offs, pos1, pos2, out):
                             start=(g == 0),
                             stop=(g == 1),
                         )
-                first = pr - 1 if pr % 2 == 1 and pr < PAIRS - 1 else pr
-                if h == 0 and (pr % 2 == 1 or pr == PAIRS - 2):
-                    copy = nc.vector.tensor_copy if pr == PAIRS - 1 else nc.scalar.copy
-                    src = last[h][:] if pr == PAIRS - 1 else acc[h][pr // 2][:, (first % 2) * 2 * C : (pr % 2 + 1) * 2 * C]
-                    copy(out=y[h][:, first * 2 * C : (pr + 1) * 2 * C], in_=src)
+
+        def empty(h, q):
+            n = 4 * C if q < E // 4 - 1 else 2 * C
+            nc.scalar.copy(out=y[h][:, q * 4 * C : q * 4 * C + n], in_=acc[h][q][:, 0:n])
 
         waiting = []
         quantized = []
@@ -139,7 +156,7 @@ def tile_routed_moe_kernel(tc, xT, w, gate, offs, pos1, pos2, out):
         def multiply_ready():
             for pr in list(waiting):
                 if pr // 2 in quantized:
-                    multiply(pr)
+                    multiply(pr, (0,) if pr in HSPLIT else (0, 1))
                     waiting.remove(pr)
 
         for t in range(4):
@@ -158,14 +175,23 @@ def tile_routed_moe_kernel(tc, xT, w, gate, offs, pos1, pos2, out):
             multiply_ready()
             if r - 1 < PAIRS:
                 interleave_weights(r - 1)
+            if r >= PC_LAG and (r - PC_LAG) % 2 == 0 and (r - PC_LAG) // 2 < 2:
+                empty(0, (r - PC_LAG) // 2)
             if r < len(UNITS):
                 for t in range(4):
                     gather(r, t)
         multiply_ready()
         assert not waiting
-        for q in range(1, E // 4 - 1):
-            nc.scalar.copy(out=y[1][:, q * 4 * C : (q + 1) * 4 * C], in_=acc[1][q][:])
-        nc.scalar.copy(out=y[1][:, 12 * C : 14 * C], in_=acc[1][3][:, 0 : 2 * C])
+        empty(0, 2)
+        empty(0, 3)
+        nc.vector.tensor_copy(out=y[0][:, 14 * C : 16 * C], in_=last[0][:])
+        for pr in HSPLIT:
+            interleave_weights(pr, 1)
+        for pr in HSPLIT:
+            quantize_weights(pr, 1)
+            multiply(pr, (1,))
+        for q in range(1, E // 4):
+            empty(1, q)
         nc.scalar.copy(out=y[1][:, 14 * C : 16 * C], in_=last[1][:])
 
         steps = []

@@ -55,15 +55,10 @@ def tile_routed_moe_kernel(tc, xT, w, gate, offs, pos1, pos2, out):
             elif what[0] == "w":
                 pr = int(what[1])
                 if pr not in wr:
-                    wr[pr] = raw.tile([P, 4, 4 * N], F32, name="wr%d" % pr, tag="raw")
+                    wr[pr] = raw.tile([P, 4, 4, N], F32, name="wr%d" % pr, tag="raw")
                 for i in [0] if what[2:] == "a" else [1] if what[2:] == "b" else [0, 1]:
                     for g in range(2):
-                        if pr in HSPLIT:
-                            for h in range(2):
-                                m0 = ((2 * h + i) * 2 + g) * P
-                                nc.sync.dma_start(out=wr[pr][:, :, m0 : m0 + P], in_=wv[2 * pr + i, g][:, :, h * P : (h + 1) * P])
-                        else:
-                            nc.sync.dma_start(out=wr[pr][:, :, (2 * i + g) * N : (2 * i + g + 1) * N], in_=wv[2 * pr + i, g])
+                        nc.sync.dma_start(out=wr[pr][:, 2 * i + g], in_=wv[2 * pr + i, g])
             else:
                 gt = raw.tile([P, 2, 2, T], F32, name="gt", tag="raw")
                 for h in range(2):
@@ -105,14 +100,24 @@ def tile_routed_moe_kernel(tc, xT, w, gate, offs, pos1, pos2, out):
         def quantize_tokens(c):
             nc.vector.quantize_mx(out=tcod[c][:].bitcast(FP8X4), scales=tscl[c][:], in_=tb[c][:].rearrange("p g n t -> p (g n t)"))
 
+        def interleave_blocks(copy, pr, m0, n0, n, b0, b1):
+            copy(
+                out=wb[pr][:, m0 : m0 + (b1 - b0) * n, :].rearrange("p (b c i) j -> p b c j i", b=b1 - b0, i=4),
+                in_=wr[pr][:, b0:b1, :, n0 : n0 + n].rearrange("p b j (c i) -> p b c j i", i=4),
+            )
+
         def interleave_weights(pr, half=0):
             if half == 0:
                 wb[pr] = stage.tile([P, 4 * N, 4], BF16, name="wb", tag="wb", bufs=WB_BUFS, align_bytes=64)
-            if pr in HSPLIT:
-                cols = slice(half * 2 * N, (half + 1) * 2 * N)
-                interleave(wb[pr][:, cols, :], wr[pr][:, :, cols], 2 * N, WSPLIT[pr] if half == 0 else 0)
-            else:
-                interleave(wb[pr][:], wr[pr][:], 4 * N, WSPLIT[pr], WPIECES[pr])
+            n = P if pr in HSPLIT else N
+            m0, n0 = (half * 2 * N, half * P) if pr in HSPLIT else (0, 0)
+            b_vector = (WSPLIT[pr] if half == 0 else 0) // n
+            b_scalar = 4 - b_vector
+            for k in range(WPIECES[pr]):
+                b0, b1 = k * b_scalar // WPIECES[pr], (k + 1) * b_scalar // WPIECES[pr]
+                interleave_blocks(nc.scalar.copy, pr, m0 + b0 * n, n0, n, b0, b1)
+            if b_vector:
+                interleave_blocks(nc.vector.tensor_copy, pr, m0 + b_scalar * n, n0, n, b_scalar, 4)
 
         def quantize_weights(pr, half=0):
             if half == 0:

@@ -13,22 +13,19 @@ U8 = mybir.dt.uint8
 FP8X4 = mybir.dt.float8_e4m3fn_x4
 MULT = mybir.AluOpType.mult
 ADD = mybir.AluOpType.add
+COPY = mybir.ActivationFunctionType.Copy
 
 P = 128
 CH = 512
 PAIRS = E // 2
-RAW_BUFS = 3
-G4_BUFS = 3
+RAW_BUFS = 4
 WB_BUFS = 3
-LOADS = ["x00", "x01", "x02", "w0a", "x03", "w0b", "x10", "x11", "x12", "x13"] + ["w%d" % pr for pr in range(1, 8)] + ["g"]
-UNITS = [(0, 0), (1, 0), (0, 1), (1, 1), (2, 0), (2, 1), (3, 0), (3, 1)]
-WSPLIT = [0, 0, 0, 0, 0, 0, 0, 256]
-TSPLIT = [0, 0, 0, 0, 0, 0, 0, 256]
-TOKS = [[1024], [768, 256]]
-WPIECES = [2, 1, 1, 1, 1, 1, 1, 1]
 WQ_BUFS = 4
-PC_LAG = 6
-HSPLIT = [6, 7]
+TB_BUFS = 4
+TC_BUFS = 1
+STOK = ["F0", "F1", "I0", "I1", "F2", "I2", "F3", "I3"]
+VBLOCKS = [4, 4, 4, 4, 4, 4, 2, 2]
+TOKS = [[1024], [768, 256]]
 
 
 def tile_routed_moe_kernel(tc, xT, w, gate, offs, pos1, pos2, out):
@@ -37,8 +34,7 @@ def tile_routed_moe_kernel(tc, xT, w, gate, offs, pos1, pos2, out):
         lists = ctx.enter_context(tc.tile_pool(name="lists", bufs=1))
         raw = ctx.enter_context(tc.tile_pool(name="raw", bufs=RAW_BUFS))
         keep = ctx.enter_context(tc.tile_pool(name="keep", bufs=1))
-        stage = ctx.enter_context(tc.tile_pool(name="stage", bufs=2))
-        fin = ctx.enter_context(tc.tile_pool(name="fin", bufs=2))
+        stage = ctx.enter_context(tc.tile_pool(name="stage", bufs=1))
         psum = ctx.enter_context(tc.psum_pool(name="psum", bufs=1))
 
         offs_sb = lists.tile([P, E * C // 16], U16, name="offs_sb")
@@ -46,23 +42,23 @@ def tile_routed_moe_kernel(tc, xT, w, gate, offs, pos1, pos2, out):
         xv = xT.rearrange("(g p t) n -> g p t n", p=P, t=4)
         wv = w.rearrange("e (g p j) n -> e g p j n", g=2, p=P, j=4)
         gv = gate.rearrange("r (h p) t -> h p r t", p=P)
-        xp, wr = {}, {}
-        for what in LOADS:
-            if what[0] == "x":
-                g, t = int(what[1]), int(what[2])
-                xp[g, t] = keep.tile([P, T], F32, name="xp%d%d" % (g, t))
-                nc.sync.dma_start(out=xp[g, t][:], in_=xv[g, :, t, :])
-            elif what[0] == "w":
-                pr = int(what[1])
-                if pr not in wr:
-                    wr[pr] = raw.tile([P, 4, 4, N], F32, name="wr%d" % pr, tag="raw")
-                for i in [0] if what[2:] == "a" else [1] if what[2:] == "b" else [0, 1]:
-                    for g in range(2):
-                        nc.sync.dma_start(out=wr[pr][:, 2 * i + g], in_=wv[2 * pr + i, g])
-            else:
-                gt = raw.tile([P, 2, 2, T], F32, name="gt", tag="raw")
-                for h in range(2):
-                    nc.sync.dma_start(out=gt[:, h], in_=gv[h])
+        xp = [keep.tile([P, T], F32, name="xp%d" % t) for t in range(4)]
+        x1 = raw.tile([P, 4, T], F32, name="x1", tag="raw")
+        xb = keep.tile([P, 4, T], BF16, name="xb")
+        nc.sync.dma_start(out=xp[0][:], in_=xv[0, :, 0, :])
+        for t in range(4):
+            nc.sync.dma_start(out=x1[:, t, :], in_=xv[1, :, t, :])
+        for t in range(1, 4):
+            nc.sync.dma_start(out=xp[t][:], in_=xv[0, :, t, :])
+        wr = {}
+        for pr in range(PAIRS):
+            wr[pr] = raw.tile([P, 4, 4, N], F32, name="wr%d" % pr, tag="raw")
+            for i in range(2):
+                for g in range(2):
+                    nc.sync.dma_start(out=wr[pr][:, 2 * i + g], in_=wv[2 * pr + i, g])
+        gt = raw.tile([P, 2, 2, T], F32, name="gt", tag="raw")
+        for h in range(2):
+            nc.sync.dma_start(out=gt[:, h], in_=gv[h])
         pos_sb = []
         for r, lst in enumerate((pos1, pos2)):
             pos_sb.append(lists.tile([P, T // 16], U16, name="pos_sb%d" % r))
@@ -70,135 +66,101 @@ def tile_routed_moe_kernel(tc, xT, w, gate, offs, pos1, pos2, out):
 
         y = [keep.tile([P, E * C], F32, name="y%d" % h) for h in range(2)]
         acc = [[psum.tile([P, 4 * C], F32, name="acc%d_%d" % (h, q)) for q in range(E // 4)] for h in range(2)]
-        last = {}
-        tcod = [keep.tile([P, 2 * CH], U32, name="tcod%d" % c, align_bytes=64) for c in range(4)]
-        tscl = [keep.tile([P, 2 * CH], U8, name="tscl%d" % c, align_bytes=64) for c in range(4)]
-        g4, tb, wb, wcod, wscl = {}, {}, {}, {}, {}
+        g4, tb, tcod, tscl, wb, wcod, wscl = {}, {}, {}, {}, {}, {}, {}
 
-        def interleave(dst, src, n, n_vector, pieces=1):
-            n_scalar = n - n_vector
-            shares = [(nc.scalar.copy, k * n_scalar // pieces, (k + 1) * n_scalar // pieces) for k in range(pieces)]
-            for copy, lo, hi in shares + [(nc.vector.tensor_copy, n_scalar, n)]:
-                if hi > lo:
-                    copy(
-                        out=dst[:, lo:hi, :].rearrange("p (c i) j -> p c j i", i=4),
-                        in_=src[:, :, lo:hi].rearrange("p j (c i) -> p c j i", i=4),
+        def gather0(gst, c):
+            g4[c] = gst.tile([P, 4, CH], F32, name="g4_%d" % c)
+            for t in range(4):
+                nc.vector.tensor_copy(g4[c][:, t, :], xp[t][:].indirect(offs_sb[:, c * (CH // 16) : (c + 1) * (CH // 16)]))
+
+        def token_tile(c):
+            if c not in tb:
+                tb[c] = stage.tile([P, 2, CH, 4], BF16, name="tb", tag="tb", bufs=TB_BUFS, align_bytes=64)
+
+        def interleave0(c):
+            token_tile(c)
+            nc.scalar.copy(
+                out=tb[c][:, 0].rearrange("p (c i) j -> p c j i", i=4),
+                in_=g4[c][:].rearrange("p j (c i) -> p c j i", i=4),
+            )
+
+        def gather1(c):
+            token_tile(c)
+            for e in range(4 * c, 4 * c + 4):
+                s0 = (e % 4) * C
+                for t in range(4):
+                    nc.scalar.activation(
+                        tb[c][:, 1, s0 : s0 + C, t], xb[:, t, :].indirect(offs_sb[:, e * (C // 16) : (e + 1) * (C // 16)]), COPY
                     )
 
-        def gather(u, t):
-            c, g = UNITS[u]
-            if t == 0:
-                g4[u] = stage.tile([P, 4, CH], F32, name="g4", tag="g4", bufs=G4_BUFS)
-            nc.vector.tensor_copy(g4[u][:, t, :], xp[g, t][:].indirect(offs_sb[:, c * (CH // 16) : (c + 1) * (CH // 16)]))
-
-        def interleave_tokens(u):
-            c, g = UNITS[u]
-            if c not in tb:
-                tb[c] = stage.tile([P, 2, CH, 4], BF16, name="tb", tag="tb", align_bytes=64)
-            interleave(tb[c][:, g], g4[u][:], CH, TSPLIT[u])
-
         def quantize_tokens(c):
+            tcod[c] = stage.tile([P, 2 * CH], U32, name="tcod", tag="tcod", bufs=TC_BUFS, align_bytes=64)
+            tscl[c] = stage.tile([P, 2 * CH], U8, name="tscl", tag="tscl", bufs=TC_BUFS, align_bytes=64)
             nc.vector.quantize_mx(out=tcod[c][:].bitcast(FP8X4), scales=tscl[c][:], in_=tb[c][:].rearrange("p g n t -> p (g n t)"))
 
-        def interleave_blocks(copy, pr, m0, n0, n, b0, b1):
+        def interleave_blocks(copy, pr, b0, b1):
             copy(
-                out=wb[pr][:, m0 : m0 + (b1 - b0) * n, :].rearrange("p (b c i) j -> p b c j i", b=b1 - b0, i=4),
-                in_=wr[pr][:, b0:b1, :, n0 : n0 + n].rearrange("p b j (c i) -> p b c j i", i=4),
+                out=wb[pr][:, b0 * N : b1 * N, :].rearrange("p (b c i) j -> p b c j i", b=b1 - b0, i=4),
+                in_=wr[pr][:, b0:b1, :, :].rearrange("p b j (c i) -> p b c j i", i=4),
             )
 
-        def interleave_weights(pr, half=0):
-            if half == 0:
-                wb[pr] = stage.tile([P, 4 * N, 4], BF16, name="wb", tag="wb", bufs=WB_BUFS, align_bytes=64)
-            n = P if pr in HSPLIT else N
-            m0, n0 = (half * 2 * N, half * P) if pr in HSPLIT else (0, 0)
-            b_vector = (WSPLIT[pr] if half == 0 else 0) // n
-            b_scalar = 4 - b_vector
-            for k in range(WPIECES[pr]):
-                b0, b1 = k * b_scalar // WPIECES[pr], (k + 1) * b_scalar // WPIECES[pr]
-                interleave_blocks(nc.scalar.copy, pr, m0 + b0 * n, n0, n, b0, b1)
-            if b_vector:
-                interleave_blocks(nc.vector.tensor_copy, pr, m0 + b_scalar * n, n0, n, b_scalar, 4)
+        def interleave_weights(pr):
+            wb[pr] = stage.tile([P, 4 * N, 4], BF16, name="wb", tag="wb", bufs=WB_BUFS, align_bytes=64)
+            nv = VBLOCKS[pr]
+            ns = 4 - nv
+            if ns:
+                interleave_blocks(nc.scalar.copy, pr, 0, ns)
+            if nv % 2:
+                interleave_blocks(nc.vector.tensor_copy, pr, ns, ns + 1)
+            if nv >= 2:
+                interleave_blocks(nc.vector.tensor_copy, pr, ns + nv % 2, 4)
 
-        def quantize_weights(pr, half=0):
-            if half == 0:
-                wcod[pr] = stage.tile([P, 4 * N], U32, name="wcod", tag="wcod", bufs=WQ_BUFS, align_bytes=64)
-                wscl[pr] = stage.tile([P, 4 * N], U8, name="wscl", tag="wscl", bufs=WQ_BUFS, align_bytes=64)
-            cols = slice(half * 2 * N, (half + 1) * 2 * N) if pr in HSPLIT else slice(0, 4 * N)
-            nc.vector.quantize_mx(
-                out=wcod[pr][:, cols].bitcast(FP8X4), scales=wscl[pr][:, cols], in_=wb[pr][:, cols, :].rearrange("p m j -> p (m j)")
-            )
+        def quantize_weights(pr):
+            wcod[pr] = stage.tile([P, 4 * N], U32, name="wcod", tag="wcod", bufs=WQ_BUFS, align_bytes=64)
+            wscl[pr] = stage.tile([P, 4 * N], U8, name="wscl", tag="wscl", bufs=WQ_BUFS, align_bytes=64)
+            nc.vector.quantize_mx(out=wcod[pr][:].bitcast(FP8X4), scales=wscl[pr][:], in_=wb[pr][:].rearrange("p m j -> p (m j)"))
 
-        def multiply(pr, halves=(0, 1)):
-            for h in halves:
-                if pr == PAIRS - 1:
-                    if h == 1:
-                        empty(1, 0)
-                    last[h] = psum.tile([P, 2 * C], F32, name="last%d" % h, tag="acc%d_0" % h)
+        def multiply(pr):
+            for h in range(2):
                 for i in range(2):
                     e = 2 * pr + i
                     c, s0 = e // 4, (e % 4) * C
                     for g in range(2):
-                        w0 = ((2 * h + i) * 2 + g) * P if pr in HSPLIT else (2 * i + g) * N + h * P
-                        wcols = slice(w0, w0 + P)
-                        tcols = slice(g * CH + s0, g * CH + s0 + C)
+                        w0 = (2 * i + g) * N + h * P
                         nc.tensor.matmul_mx(
-                            out=last[h][:, i * C : (i + 1) * C] if pr == PAIRS - 1 else acc[h][c][:, s0 : s0 + C],
-                            lhsT=wcod[pr][:, wcols].bitcast(FP8X4),
-                            lhsT_scale=wscl[pr][:, wcols],
-                            rhs=tcod[c][:, tcols].bitcast(FP8X4),
-                            rhs_scale=tscl[c][:, tcols],
+                            out=acc[h][c][:, s0 : s0 + C],
+                            lhsT=wcod[pr][:, w0 : w0 + P].bitcast(FP8X4),
+                            lhsT_scale=wscl[pr][:, w0 : w0 + P],
+                            rhs=tcod[c][:, g * CH + s0 : g * CH + s0 + C].bitcast(FP8X4),
+                            rhs_scale=tscl[c][:, g * CH + s0 : g * CH + s0 + C],
                             start=(g == 0),
                             stop=(g == 1),
                         )
 
         def empty(h, q):
-            n = 4 * C if q < E // 4 - 1 else 2 * C
-            nc.scalar.copy(out=y[h][:, q * 4 * C : q * 4 * C + n], in_=acc[h][q][:, 0:n])
-
-        waiting = []
-        quantized = []
-
-        def multiply_ready():
-            for pr in list(waiting):
-                if pr // 2 in quantized:
-                    multiply(pr, (0,) if pr in HSPLIT else (0, 1))
-                    waiting.remove(pr)
+            nc.scalar.copy(out=y[h][:, q * 4 * C : (q + 1) * 4 * C], in_=acc[h][q][:])
 
         for t in range(4):
-            gather(0, t)
-            gather(1, t)
-        interleave_weights(0)
-        for r in range(2, len(UNITS) + 2):
-            for u in [0, 1] if r == 2 else [r - 1] if r <= len(UNITS) else []:
-                interleave_tokens(u)
-                if UNITS[u][1] == 1:
-                    quantize_tokens(UNITS[u][0])
-                    quantized.append(UNITS[u][0])
-            if r - 2 < PAIRS:
-                quantize_weights(r - 2)
-                waiting.append(r - 2)
-            multiply_ready()
-            if r - 1 < PAIRS:
-                interleave_weights(r - 1)
-            if r >= PC_LAG and (r - PC_LAG) % 2 == 0 and (r - PC_LAG) // 2 < 2:
-                empty(0, (r - PC_LAG) // 2)
-            if r < len(UNITS):
-                for t in range(4):
-                    gather(r, t)
-        multiply_ready()
-        assert not waiting
-        empty(0, 2)
-        empty(0, 3)
-        nc.vector.tensor_copy(out=y[0][:, 14 * C : 16 * C], in_=last[0][:])
-        for pr in HSPLIT:
-            interleave_weights(pr, 1)
-        for pr in HSPLIT:
-            quantize_weights(pr, 1)
-            multiply(pr, (1,))
-        for q in range(1, E // 4):
-            empty(1, q)
-        nc.scalar.copy(out=y[1][:, 14 * C : 16 * C], in_=last[1][:])
+            nc.scalar.copy(out=xb[:, t, :], in_=x1[:, t, :])
+        with tc.tile_pool(name="gst", bufs=1) as gst:
+            for c in range(4):
+                gather0(gst, c)
+            for op in STOK:
+                if op[0] == "F":
+                    gather1(int(op[1]))
+                else:
+                    interleave0(int(op[1]))
+            for c in range(4):
+                quantize_tokens(c)
+                for pr in (2 * c, 2 * c + 1):
+                    interleave_weights(pr)
+                    quantize_weights(pr)
+                    multiply(pr)
+        for h in range(2):
+            for q in range(E // 4):
+                empty(h, q)
 
+        fin = ctx.enter_context(tc.tile_pool(name="fin", bufs=2))
         steps = []
         for h in range(2):
             t0 = 0

@@ -22,9 +22,10 @@ RAW_BUFS = 4
 WB_BUFS = 3
 WQ_BUFS = 4
 TB_BUFS = 4
-TC_BUFS = 1
-STOK = ["F0", "F1", "I0", "I1", "F2", "I2", "F3", "I3"]
+TC_BUFS = 2
+STOK = [("F", 0, 0, 4), ("F", 1, 0, 3), ("I", 0), ("F", 1, 3, 4), ("I", 1), ("F", 2, 0, 4), ("I", 2), ("F", 3, 0, 4), ("I", 3)]
 VBLOCKS = [4, 4, 4, 4, 4, 4, 2, 2]
+HELD = 3
 TOKS = [[1024], [768, 256]]
 
 
@@ -53,9 +54,12 @@ def tile_routed_moe_kernel(tc, xT, w, gate, offs, pos1, pos2, out):
         wr = {}
         for pr in range(PAIRS):
             wr[pr] = raw.tile([P, 4, 4, N], F32, name="wr%d" % pr, tag="raw")
-            for i in range(2):
-                for g in range(2):
-                    nc.sync.dma_start(out=wr[pr][:, 2 * i + g], in_=wv[2 * pr + i, g])
+            for b in range(4):
+                if b < 3 or pr >= HELD:
+                    nc.sync.dma_start(out=wr[pr][:, b], in_=wv[2 * pr + b // 2, b % 2])
+            if pr == HELD - 1:
+                for held in range(HELD):
+                    nc.sync.dma_start(out=wr[held][:, 3], in_=wv[2 * held + 1, 1])
         gt = raw.tile([P, 2, 2, T], F32, name="gt", tag="raw")
         for h in range(2):
             nc.sync.dma_start(out=gt[:, h], in_=gv[h])
@@ -75,28 +79,32 @@ def tile_routed_moe_kernel(tc, xT, w, gate, offs, pos1, pos2, out):
 
         def token_tile(c):
             if c not in tb:
-                tb[c] = stage.tile([P, 2, CH, 4], BF16, name="tb", tag="tb", bufs=TB_BUFS, align_bytes=64)
+                tb[c] = stage.tile([P, 2, 2, 2 * C, 4], BF16, name="tb", tag="tb", bufs=TB_BUFS, align_bytes=64)
 
         def interleave0(c):
             token_tile(c)
             nc.scalar.copy(
-                out=tb[c][:, 0].rearrange("p (c i) j -> p c j i", i=4),
-                in_=g4[c][:].rearrange("p j (c i) -> p c j i", i=4),
+                out=tb[c][:, :, 0].rearrange("p a (c i) j -> p a c j i", i=4),
+                in_=g4[c][:].rearrange("p j (a c i) -> p a c j i", a=2, i=4),
             )
 
-        def gather1(c):
+        def gather1(c, lo, hi):
             token_tile(c)
-            for e in range(4 * c, 4 * c + 4):
-                s0 = (e % 4) * C
+            for e in range(4 * c + lo, 4 * c + hi):
+                s0 = (e % 2) * C
                 for t in range(4):
                     nc.scalar.activation(
-                        tb[c][:, 1, s0 : s0 + C, t], xb[:, t, :].indirect(offs_sb[:, e * (C // 16) : (e + 1) * (C // 16)]), COPY
+                        tb[c][:, (e % 4) // 2, 1, s0 : s0 + C, t],
+                        xb[:, t, :].indirect(offs_sb[:, e * (C // 16) : (e + 1) * (C // 16)]),
+                        COPY,
                     )
 
-        def quantize_tokens(c):
-            tcod[c] = stage.tile([P, 2 * CH], U32, name="tcod", tag="tcod", bufs=TC_BUFS, align_bytes=64)
-            tscl[c] = stage.tile([P, 2 * CH], U8, name="tscl", tag="tscl", bufs=TC_BUFS, align_bytes=64)
-            nc.vector.quantize_mx(out=tcod[c][:].bitcast(FP8X4), scales=tscl[c][:], in_=tb[c][:].rearrange("p g n t -> p (g n t)"))
+        def quantize_tokens(pr):
+            tcod[pr] = stage.tile([P, 4 * C], U32, name="tcod", tag="tcod", bufs=TC_BUFS, align_bytes=64)
+            tscl[pr] = stage.tile([P, 4 * C], U8, name="tscl", tag="tscl", bufs=TC_BUFS, align_bytes=64)
+            nc.vector.quantize_mx(
+                out=tcod[pr][:].bitcast(FP8X4), scales=tscl[pr][:], in_=tb[pr // 2][:, pr % 2].rearrange("p g n t -> p (g n t)")
+            )
 
         def interleave_blocks(copy, pr, b0, b1):
             copy(
@@ -131,8 +139,8 @@ def tile_routed_moe_kernel(tc, xT, w, gate, offs, pos1, pos2, out):
                             out=acc[h][c][:, s0 : s0 + C],
                             lhsT=wcod[pr][:, w0 : w0 + P].bitcast(FP8X4),
                             lhsT_scale=wscl[pr][:, w0 : w0 + P],
-                            rhs=tcod[c][:, g * CH + s0 : g * CH + s0 + C].bitcast(FP8X4),
-                            rhs_scale=tscl[c][:, g * CH + s0 : g * CH + s0 + C],
+                            rhs=tcod[pr][:, (2 * g + i) * C : (2 * g + i + 1) * C].bitcast(FP8X4),
+                            rhs_scale=tscl[pr][:, (2 * g + i) * C : (2 * g + i + 1) * C],
                             start=(g == 0),
                             stop=(g == 1),
                         )
@@ -147,15 +155,19 @@ def tile_routed_moe_kernel(tc, xT, w, gate, offs, pos1, pos2, out):
                 gather0(gst, c)
             for op in STOK:
                 if op[0] == "F":
-                    gather1(int(op[1]))
+                    gather1(op[1], op[2], op[3])
                 else:
-                    interleave0(int(op[1]))
-            for c in range(4):
-                quantize_tokens(c)
-                for pr in (2 * c, 2 * c + 1):
-                    interleave_weights(pr)
-                    quantize_weights(pr)
-                    multiply(pr)
+                    interleave0(op[1])
+            for pr in range(2):
+                quantize_tokens(pr)
+            for pr in range(2):
+                interleave_weights(pr)
+            for pr in range(PAIRS):
+                quantize_weights(pr)
+                multiply(pr)
+                if pr + 2 < PAIRS:
+                    interleave_weights(pr + 2)
+                    quantize_tokens(pr + 2)
         for h in range(2):
             for q in range(E // 4):
                 empty(h, q)

@@ -25,6 +25,8 @@ TB_BUFS = 4
 TC_BUFS = 2
 STOK = [("F", 0, 0, 4), ("F", 1, 0, 3), ("I", 0), ("F", 1, 3, 4), ("I", 1), ("F", 2, 0, 4), ("I", 2), ("F", 3, 0, 4), ("I", 3)]
 VBLOCKS = [4, 4, 4, 4, 4, 4, 2, 2]
+HS = [6, 7]
+XLOADS = [(0, 0), (1, 0), (1, 1), (1, 2), (0, 1), (1, 3), (0, 2), (0, 3)]
 HELD = 3
 TOKS = [[1024], [768, 256]]
 
@@ -46,11 +48,8 @@ def tile_routed_moe_kernel(tc, xT, w, gate, offs, pos1, pos2, out):
         xp = [keep.tile([P, T], F32, name="xp%d" % t) for t in range(4)]
         x1 = raw.tile([P, 4, T], F32, name="x1", tag="raw")
         xb = keep.tile([P, 4, T], BF16, name="xb")
-        nc.sync.dma_start(out=xp[0][:], in_=xv[0, :, 0, :])
-        for t in range(4):
-            nc.sync.dma_start(out=x1[:, t, :], in_=xv[1, :, t, :])
-        for t in range(1, 4):
-            nc.sync.dma_start(out=xp[t][:], in_=xv[0, :, t, :])
+        for g, t in XLOADS:
+            nc.sync.dma_start(out=x1[:, t, :] if g else xp[t][:], in_=xv[g, :, t, :])
         wr = {}
         for pr in range(PAIRS):
             wr[pr] = raw.tile([P, 4, 4, N], F32, name="wr%d" % pr, tag="raw")
@@ -106,35 +105,41 @@ def tile_routed_moe_kernel(tc, xT, w, gate, offs, pos1, pos2, out):
                 out=tcod[pr][:].bitcast(FP8X4), scales=tscl[pr][:], in_=tb[pr // 2][:, pr % 2].rearrange("p g n t -> p (g n t)")
             )
 
-        def interleave_blocks(copy, pr, b0, b1):
+        def interleave_blocks(copy, pr, b0, b1, m0, n0, n):
             copy(
-                out=wb[pr][:, b0 * N : b1 * N, :].rearrange("p (b c i) j -> p b c j i", b=b1 - b0, i=4),
-                in_=wr[pr][:, b0:b1, :, :].rearrange("p b j (c i) -> p b c j i", i=4),
+                out=wb[pr][:, m0 + b0 * n : m0 + b1 * n, :].rearrange("p (b c i) j -> p b c j i", b=b1 - b0, i=4),
+                in_=wr[pr][:, b0:b1, :, n0 : n0 + n].rearrange("p b j (c i) -> p b c j i", i=4),
             )
 
-        def interleave_weights(pr):
-            wb[pr] = stage.tile([P, 4 * N, 4], BF16, name="wb", tag="wb", bufs=WB_BUFS, align_bytes=64)
-            nv = VBLOCKS[pr]
+        def interleave_weights(pr, half=0):
+            if half == 0:
+                wb[pr] = stage.tile([P, 4 * N, 4], BF16, name="wb", tag="wb", bufs=WB_BUFS, align_bytes=64)
+            m0, n0, n = (half * 2 * N, half * P, P) if pr in HS else (0, 0, N)
+            nv = VBLOCKS[pr] if half == 0 else 0
             ns = 4 - nv
             if ns:
-                interleave_blocks(nc.scalar.copy, pr, 0, ns)
+                interleave_blocks(nc.scalar.copy, pr, 0, ns, m0, n0, n)
             if nv % 2:
-                interleave_blocks(nc.vector.tensor_copy, pr, ns, ns + 1)
+                interleave_blocks(nc.vector.tensor_copy, pr, ns, ns + 1, m0, n0, n)
             if nv >= 2:
-                interleave_blocks(nc.vector.tensor_copy, pr, ns + nv % 2, 4)
+                interleave_blocks(nc.vector.tensor_copy, pr, ns + nv % 2, 4, m0, n0, n)
 
-        def quantize_weights(pr):
-            wcod[pr] = stage.tile([P, 4 * N], U32, name="wcod", tag="wcod", bufs=WQ_BUFS, align_bytes=64)
-            wscl[pr] = stage.tile([P, 4 * N], U8, name="wscl", tag="wscl", bufs=WQ_BUFS, align_bytes=64)
-            nc.vector.quantize_mx(out=wcod[pr][:].bitcast(FP8X4), scales=wscl[pr][:], in_=wb[pr][:].rearrange("p m j -> p (m j)"))
+        def quantize_weights(pr, half=0):
+            if half == 0:
+                wcod[pr] = stage.tile([P, 4 * N], U32, name="wcod", tag="wcod", bufs=WQ_BUFS, align_bytes=64)
+                wscl[pr] = stage.tile([P, 4 * N], U8, name="wscl", tag="wscl", bufs=WQ_BUFS, align_bytes=64)
+            cols = slice(half * 2 * N, (half + 1) * 2 * N) if pr in HS else slice(0, 4 * N)
+            nc.vector.quantize_mx(
+                out=wcod[pr][:, cols].bitcast(FP8X4), scales=wscl[pr][:, cols], in_=wb[pr][:, cols, :].rearrange("p m j -> p (m j)")
+            )
 
-        def multiply(pr):
-            for h in range(2):
+        def multiply(pr, halves=(0, 1)):
+            for h in halves:
                 for i in range(2):
                     e = 2 * pr + i
                     c, s0 = e // 4, (e % 4) * C
                     for g in range(2):
-                        w0 = (2 * i + g) * N + h * P
+                        w0 = ((2 * h + i) * 2 + g) * P if pr in HS else (2 * i + g) * N + h * P
                         nc.tensor.matmul_mx(
                             out=acc[h][c][:, s0 : s0 + C],
                             lhsT=wcod[pr][:, w0 : w0 + P].bitcast(FP8X4),
@@ -164,13 +169,19 @@ def tile_routed_moe_kernel(tc, xT, w, gate, offs, pos1, pos2, out):
                 interleave_weights(pr)
             for pr in range(PAIRS):
                 quantize_weights(pr)
-                multiply(pr)
+                multiply(pr, (0,) if pr in HS else (0, 1))
                 if pr + 2 < PAIRS:
                     interleave_weights(pr + 2)
                     quantize_tokens(pr + 2)
-        for h in range(2):
             for q in range(E // 4):
-                empty(h, q)
+                empty(0, q)
+            for pr in HS:
+                interleave_weights(pr, 1)
+            for pr in HS:
+                quantize_weights(pr, 1)
+                multiply(pr, (1,))
+        for q in range(E // 4):
+            empty(1, q)
 
         fin = ctx.enter_context(tc.tile_pool(name="fin", bufs=2))
         steps = []

@@ -24,7 +24,7 @@ WQ_BUFS = 4
 TB_BUFS = 4
 TC_BUFS = 2
 STOK = [("F", 0, 0, 4), ("F", 1, 0, 3), ("I", 0), ("F", 1, 3, 4), ("I", 1), ("F", 2, 0, 4), ("I", 2), ("F", 3, 0, 4), ("I", 3)]
-VBLOCKS = [4, 4, 4, 4, 4, 4, 2, 2]
+VBLOCKS = [4, 4, 4, 4, 4, 4, 4, 4]
 HS = [6, 7]
 XLOADS = [(0, 0), (1, 0), (1, 1), (1, 2), (0, 1), (1, 3), (0, 2), (0, 3)]
 HELD = 3

@@ -1,6 +1,7 @@
 from contextlib import ExitStack
 
 import concourse.mybir as mybir
+from concourse.masks import make_identity
 
 K, T, E, C, N = 1024, 1024, 16, 128, 256
 FLOPS = 2 * K * N * E * C
@@ -29,6 +30,7 @@ HS = [6, 7]
 XLOADS = [(0, 0), (1, 0), (1, 1), (1, 2), (0, 1), (1, 3), (0, 2), (0, 3)]
 HELD = 3
 TOKS = [[1024], [768, 256]]
+PE_ADDS = 1
 
 
 def tile_routed_moe_kernel(tc, xT, w, gate, offs, pos1, pos2, out):
@@ -67,6 +69,8 @@ def tile_routed_moe_kernel(tc, xT, w, gate, offs, pos1, pos2, out):
             pos_sb.append(lists.tile([P, T // 16], U16, name="pos_sb%d" % r))
             nc.sync.dma_start(pos_sb[r][:], lst)
 
+        ident = keep.tile([P, P], F32, name="ident")
+        make_identity(nc, ident[:])
         y = [keep.tile([P, E * C], F32, name="y%d" % h) for h in range(2)]
         acc = [[psum.tile([P, 4 * C], F32, name="acc%d_%d" % (h, q)) for q in range(E // 4)] for h in range(2)]
         g4, tb, tcod, tscl, wb, wcod, wscl = {}, {}, {}, {}, {}, {}, {}
@@ -206,8 +210,18 @@ def tile_routed_moe_kernel(tc, xT, w, gate, offs, pos1, pos2, out):
         def finish(s):
             h, t0, n = steps[s]
             o = fin.tile([P, n], F32, name="o", tag="o", bufs=3)
-            nc.vector.tensor_tensor(o[:], parts[s, 0][:], parts[s, 1][:], ADD)
-            nc.sync.dma_start(out=out[h * P : (h + 1) * P, t0 : t0 + n], in_=o[:])
+            if s < PE_ADDS:
+                blocks = range(n // 512)
+                banks = [psum.tile([P, 512], F32, name="sum%d" % k, tag="acc0_%d" % k) for k in blocks]
+                for r in range(2):
+                    for k in blocks:
+                        nc.tensor.matmul(banks[k][:], ident[:], parts[s, r][:, k * 512 : (k + 1) * 512], start=(r == 0), stop=(r == 1))
+                for k in blocks:
+                    nc.scalar.copy(out=o[:, k * 512 : (k + 1) * 512], in_=banks[k][:])
+                    nc.sync.dma_start(out=out[h * P : (h + 1) * P, t0 + k * 512 : t0 + (k + 1) * 512], in_=o[:, k * 512 : (k + 1) * 512])
+            else:
+                nc.vector.tensor_tensor(o[:], parts[s, 0][:], parts[s, 1][:], ADD)
+                nc.sync.dma_start(out=out[h * P : (h + 1) * P, t0 : t0 + n], in_=o[:])
 
         fetch(0)
         for s in range(1, len(steps)):

@@ -45,7 +45,7 @@ def tile_routed_moe_kernel(tc, xT, w, gate, offs, pos1, pos2, out):
         offs_sb = lists.tile([P, E * C // 16], U16, name="offs_sb")
         nc.sync.dma_start(offs_sb[:], offs)
         xv = xT.rearrange("(g p t) n -> g p t n", p=P, t=4)
-        wv = w.rearrange("e (g p j) n -> e g p j n", g=2, p=P, j=4)
+        we = w.rearrange("e (g p j) n -> e p g j n", g=2, p=P, j=4)
         gv = gate.rearrange("r (h p) t -> h p r t", p=P)
         xp = [keep.tile([P, T], F32, name="xp%d" % t) for t in range(4)]
         x1 = raw.tile([P, 4, T], F32, name="x1", tag="raw")
@@ -55,12 +55,14 @@ def tile_routed_moe_kernel(tc, xT, w, gate, offs, pos1, pos2, out):
         wr = {}
         for pr in range(PAIRS):
             wr[pr] = raw.tile([P, 4, 4, N], F32, name="wr%d" % pr, tag="raw")
-            for b in range(4):
-                if b < 3 or pr >= HELD:
-                    nc.sync.dma_start(out=wr[pr][:, b], in_=wv[2 * pr + b // 2, b % 2])
+            nc.sync.dma_start(out=wr[pr][:, 0:2], in_=we[2 * pr])
+            if pr >= HELD:
+                nc.sync.dma_start(out=wr[pr][:, 2:4], in_=we[2 * pr + 1])
+            else:
+                nc.sync.dma_start(out=wr[pr][:, 2], in_=we[2 * pr + 1][:, 0])
             if pr == HELD - 1:
                 for held in range(HELD):
-                    nc.sync.dma_start(out=wr[held][:, 3], in_=wv[2 * held + 1, 1])
+                    nc.sync.dma_start(out=wr[held][:, 3], in_=we[2 * held + 1][:, 1])
         gt = raw.tile([P, 2, 2, T], F32, name="gt", tag="raw")
         for h in range(2):
             nc.sync.dma_start(out=gt[:, h], in_=gv[h])

@@ -73,7 +73,7 @@ def tile_routed_moe_kernel(tc, xT, w, gate, offs, pos1, pos2, out):
 
         ident = keep.tile([P, P], F32, name="ident")
         make_identity(nc, ident[:])
-        y = [keep.tile([P, E * C], F32, name="y%d" % h) for h in range(2)]
+        y = [keep.tile([P, E * C], F32, name="y0")]
         acc = [[psum.tile([P, 4 * C], F32, name="acc%d_%d" % (h, q)) for q in range(E // 4)] for h in range(2)]
         g4, tb, tcod, tscl, wb, wcod, wscl = {}, {}, {}, {}, {}, {}, {}
 
@@ -186,6 +186,8 @@ def tile_routed_moe_kernel(tc, xT, w, gate, offs, pos1, pos2, out):
             for pr in HS:
                 quantize_weights(pr, 1)
                 multiply(pr, (1,))
+        late = [stage.tile([P, E * C], F32, name="late%d" % k, tag="wb", bufs=WB_BUFS, align_bytes=64) for k in range(3)]
+        y.append(late[2])
         for q in range(E // 4):
             empty(1, q)
 
@@ -201,9 +203,9 @@ def tile_routed_moe_kernel(tc, xT, w, gate, offs, pos1, pos2, out):
         def fetch(s):
             h, t0, n = steps[s]
             for r in range(2):
-                parts[s, r] = fin.tile([P, n], F32, name="part%d" % r, tag="part%d" % r)
+                parts[s, r] = late[r][:, 0:n] if s == 0 else fin.tile([P, n], F32, name="part%d" % r, tag="part%d" % r)[:]
                 nc.vector.tensor_tensor(
-                    parts[s, r][:],
+                    parts[s, r],
                     y[h][:].indirect(pos_sb[r][:] if n == T else pos_sb[r][:, t0 // 16 : (t0 + n) // 16]),
                     gt[:, h, r, t0 : t0 + n],
                     MULT,
@@ -220,9 +222,9 @@ def tile_routed_moe_kernel(tc, xT, w, gate, offs, pos1, pos2, out):
                         nc.tensor.matmul(banks[k][:], ident[:], parts[s, r][:, k * 512 : (k + 1) * 512], start=(r == 0), stop=(r == 1))
                 for k in blocks:
                     nc.scalar.copy(out=o[:, k * 512 : (k + 1) * 512], in_=banks[k][:])
-                    nc.sync.dma_start(out=out[h * P : (h + 1) * P, t0 + k * 512 : t0 + (k + 1) * 512], in_=o[:, k * 512 : (k + 1) * 512])
+                    nc.scalar.dma_start(out=out[h * P : (h + 1) * P, t0 + k * 512 : t0 + (k + 1) * 512], in_=o[:, k * 512 : (k + 1) * 512])
             else:
-                nc.vector.tensor_tensor(o[:], parts[s, 0][:], parts[s, 1][:], ADD)
+                nc.vector.tensor_tensor(o[:], parts[s, 0], parts[s, 1], ADD)
                 nc.sync.dma_start(out=out[h * P : (h + 1) * P, t0 : t0 + n], in_=o[:])
 
         fetch(0)

@@ -25,7 +25,8 @@ WQ_BUFS = 4
 TB_BUFS = 4
 TC_BUFS = 2
 STOK = [("F", 0, 0, 4), ("F", 1, 0, 3), ("I", 0), ("F", 1, 3, 4), ("I", 1), ("F", 2, 0, 4), ("I", 2), ("F", 3, 0, 4), ("I", 3)]
-VBLOCKS = [4, 4, 4, 4, 4, 4, 4, 4]
+VBLOCKS = [2, 4, 4, 4, 4, 4, 4, 4]
+GP = [0]
 HS = [6, 7]
 XLOADS = [(0, 0), (1, 0), (1, 1), (1, 2), (0, 1), (1, 3), (0, 2), (0, 3)]
 HELD = 3
@@ -124,7 +125,7 @@ def tile_routed_moe_kernel(tc, xT, w, gate, offs, pos1, pos2, out):
             nv = VBLOCKS[pr] if half == 0 else 0
             ns = 4 - nv
             if ns:
-                interleave_blocks(nc.scalar.copy, pr, 0, ns, m0, n0, n)
+                interleave_blocks(nc.gpsimd.tensor_copy if pr in GP else nc.scalar.copy, pr, 0, ns, m0, n0, n)
             if nv % 2:
                 interleave_blocks(nc.vector.tensor_copy, pr, ns, ns + 1, m0, n0, n)
             if nv >= 2:

@@ -45,6 +45,9 @@ def tile_routed_moe_kernel(tc, xT, w, gate, offs, pos1, pos2, out):
 
         offs_sb = lists.tile([P, E * C // 16], U16, name="offs_sb")
         nc.sync.dma_start(offs_sb[:], offs)
+        pos_sb = []
+        for r, lst in enumerate((pos1, pos2)):
+            pos_sb.append(lists.tile([P, T // 16], U16, name="pos_sb%d" % r))
         xv = xT.rearrange("(g p t) n -> g p t n", p=P, t=4)
         we = w.rearrange("e (g p j) n -> e p g j n", g=2, p=P, j=4)
         gv = gate.rearrange("r (h p) t -> h p r t", p=P)
@@ -53,6 +56,8 @@ def tile_routed_moe_kernel(tc, xT, w, gate, offs, pos1, pos2, out):
         xb = keep.tile([P, 4, T], BF16, name="xb")
         for g, t in XLOADS:
             nc.sync.dma_start(out=x1[:, t, :] if g else xp[t][:], in_=xv[g, :, t, :])
+        for r, lst in enumerate((pos1, pos2)):
+            nc.sync.dma_start(pos_sb[r][:], lst)
         wr = {}
         for pr in range(PAIRS):
             wr[pr] = raw.tile([P, 4, 4, N], F32, name="wr%d" % pr, tag="raw")
@@ -66,11 +71,8 @@ def tile_routed_moe_kernel(tc, xT, w, gate, offs, pos1, pos2, out):
                     nc.sync.dma_start(out=wr[held][:, 3], in_=we[2 * held + 1][:, 1])
         gt = raw.tile([P, 2, 2, T], F32, name="gt", tag="raw")
         for h in range(2):
-            nc.sync.dma_start(out=gt[:, h], in_=gv[h])
-        pos_sb = []
-        for r, lst in enumerate((pos1, pos2)):
-            pos_sb.append(lists.tile([P, T // 16], U16, name="pos_sb%d" % r))
-            nc.sync.dma_start(pos_sb[r][:], lst)
+            for r in range(2):
+                nc.sync.dma_start(out=gt[:, h, r], in_=gv[h][:, r])
 
         ident = keep.tile([P, P], F32, name="ident")
         make_identity(nc, ident[:])

@@ -26,6 +26,7 @@ TB_BUFS = 4
 TC_BUFS = 2
 STOK = [("F", 0, 0, 4), ("F", 1, 0, 3), ("I", 0), ("F", 1, 3, 4), ("I", 1), ("F", 2, 0, 4), ("I", 2), ("F", 3, 0, 4), ("I", 3)]
 VBLOCKS = [2, 4, 4, 4, 4, 4, 4, 4]
+RUN = 8
 GP = [0]
 HS = [6, 7]
 XLOADS = [(0, 0), (1, 0), (1, 1), (1, 2), (0, 1), (1, 3), (0, 2), (0, 3)]
@@ -92,8 +93,8 @@ def tile_routed_moe_kernel(tc, xT, w, gate, offs, pos1, pos2, out):
         def interleave0(c):
             token_tile(c)
             nc.scalar.copy(
-                out=tb[c][:, :, 0].rearrange("p a (c i) j -> p a c j i", i=4),
-                in_=g4[c][:].rearrange("p j (a c i) -> p a c j i", a=2, i=4),
+                out=tb[c][:, :, 0].rearrange("p a (c i) j -> p a c j i", i=RUN),
+                in_=g4[c][:].rearrange("p j (a c i) -> p a c j i", a=2, i=RUN),
             )
 
         def gather1(c, lo, hi):
@@ -116,8 +117,8 @@ def tile_routed_moe_kernel(tc, xT, w, gate, offs, pos1, pos2, out):
 
         def interleave_blocks(copy, pr, b0, b1, m0, n0, n):
             copy(
-                out=wb[pr][:, m0 + b0 * n : m0 + b1 * n, :].rearrange("p (b c i) j -> p b c j i", b=b1 - b0, i=4),
-                in_=wr[pr][:, b0:b1, :, n0 : n0 + n].rearrange("p b j (c i) -> p b c j i", i=4),
+                out=wb[pr][:, m0 + b0 * n : m0 + b1 * n, :].rearrange("p (b c i) j -> p b c j i", b=b1 - b0, i=RUN),
+                in_=wr[pr][:, b0:b1, :, n0 : n0 + n].rearrange("p b j (c i) -> p b c j i", i=RUN),
             )
 
         def interleave_weights(pr, half=0):

from contextlib import ExitStack

import concourse.mybir as mybir
from concourse.masks import make_identity

K, T, E, C, N = 1024, 1024, 16, 128, 256
FLOPS = 2 * K * N * E * C

F32 = mybir.dt.float32
BF16 = mybir.dt.bfloat16
U32 = mybir.dt.uint32
U16 = mybir.dt.uint16
U8 = mybir.dt.uint8
FP8X4 = mybir.dt.float8_e4m3fn_x4
MULT = mybir.AluOpType.mult
ADD = mybir.AluOpType.add
COPY = mybir.ActivationFunctionType.Copy

P = 128
CH = 512
PAIRS = E // 2
RAW_BUFS = 4
WB_BUFS = 3
WQ_BUFS = 4
TB_BUFS = 4
TC_BUFS = 2
STOK = [("F", 0, 0, 4), ("F", 1, 0, 3), ("I", 0), ("F", 1, 3, 4), ("I", 1), ("F", 2, 0, 4), ("I", 2), ("F", 3, 0, 4), ("I", 3)]
VBLOCKS = [2, 4, 4, 4, 4, 4, 4, 4]
RUN = 8
GP = [0]
HS = [6, 7]
XLOADS = [(0, 0), (1, 0), (1, 1), (1, 2), (0, 1), (1, 3), (0, 2), (0, 3)]
HELD = 3
TOKS = [[1024], [768, 256]]
PE_ADDS = 1


def tile_routed_moe_kernel(tc, xT, w, gate, offs, pos1, pos2, out):
    nc = tc.nc
    with ExitStack() as ctx:
        lists = ctx.enter_context(tc.tile_pool(name="lists", bufs=1))
        raw = ctx.enter_context(tc.tile_pool(name="raw", bufs=RAW_BUFS))
        keep = ctx.enter_context(tc.tile_pool(name="keep", bufs=1))
        stage = ctx.enter_context(tc.tile_pool(name="stage", bufs=1))
        psum = ctx.enter_context(tc.psum_pool(name="psum", bufs=1))

        offs_sb = lists.tile([P, E * C // 16], U16, name="offs_sb")
        nc.sync.dma_start(offs_sb[:], offs)
        pos_sb = []
        for r, lst in enumerate((pos1, pos2)):
            pos_sb.append(lists.tile([P, T // 16], U16, name="pos_sb%d" % r))
        xv = xT.rearrange("(g p t) n -> g p t n", p=P, t=4)
        we = w.rearrange("e (g p j) n -> e p g j n", g=2, p=P, j=4)
        gv = gate.rearrange("r (h p) t -> h p r t", p=P)
        xp = [keep.tile([P, T], F32, name="xp%d" % t) for t in range(4)]
        x1 = raw.tile([P, 4, T], F32, name="x1", tag="raw")
        xb = keep.tile([P, 4, T], BF16, name="xb")
        for g, t in XLOADS:
            nc.sync.dma_start(out=x1[:, t, :] if g else xp[t][:], in_=xv[g, :, t, :])
        for r, lst in enumerate((pos1, pos2)):
            nc.sync.dma_start(pos_sb[r][:], lst)
        wr = {}
        for pr in range(PAIRS):
            wr[pr] = raw.tile([P, 4, 4, N], F32, name="wr%d" % pr, tag="raw")
            nc.sync.dma_start(out=wr[pr][:, 0:2], in_=we[2 * pr])
            if pr >= HELD:
                nc.sync.dma_start(out=wr[pr][:, 2:4], in_=we[2 * pr + 1])
            else:
                nc.sync.dma_start(out=wr[pr][:, 2], in_=we[2 * pr + 1][:, 0])
            if pr == HELD - 1:
                for held in range(HELD):
                    nc.sync.dma_start(out=wr[held][:, 3], in_=we[2 * held + 1][:, 1])
        gt = raw.tile([P, 2, 2, T], F32, name="gt", tag="raw")
        for h in range(2):
            for r in range(2):
                nc.sync.dma_start(out=gt[:, h, r], in_=gv[h][:, r])

        ident = keep.tile([P, P], F32, name="ident")
        make_identity(nc, ident[:])
        y = [keep.tile([P, E * C], F32, name="y0")]
        acc = [[psum.tile([P, 4 * C], F32, name="acc%d_%d" % (h, q)) for q in range(E // 4)] for h in range(2)]
        g4, tb, tcod, tscl, wb, wcod, wscl = {}, {}, {}, {}, {}, {}, {}

        def gather0(gst, c):
            g4[c] = gst.tile([P, 4, CH], F32, name="g4_%d" % c)
            for t in range(4):
                nc.vector.tensor_copy(g4[c][:, t, :], xp[t][:].indirect(offs_sb[:, c * (CH // 16) : (c + 1) * (CH // 16)]))

        def token_tile(c):
            if c not in tb:
                tb[c] = stage.tile([P, 2, 2, 2 * C, 4], BF16, name="tb", tag="tb", bufs=TB_BUFS, align_bytes=64)

        def interleave0(c):
            token_tile(c)
            nc.scalar.copy(
                out=tb[c][:, :, 0].rearrange("p a (c i) j -> p a c j i", i=RUN),
                in_=g4[c][:].rearrange("p j (a c i) -> p a c j i", a=2, i=RUN),
            )

        def gather1(c, lo, hi):
            token_tile(c)
            for e in range(4 * c + lo, 4 * c + hi):
                s0 = (e % 2) * C
                for t in range(4):
                    nc.scalar.activation(
                        tb[c][:, (e % 4) // 2, 1, s0 : s0 + C, t],
                        xb[:, t, :].indirect(offs_sb[:, e * (C // 16) : (e + 1) * (C // 16)]),
                        COPY,
                    )

        def quantize_tokens(pr):
            tcod[pr] = stage.tile([P, 4 * C], U32, name="tcod", tag="tcod", bufs=TC_BUFS, align_bytes=64)
            tscl[pr] = stage.tile([P, 4 * C], U8, name="tscl", tag="tscl", bufs=TC_BUFS, align_bytes=64)
            nc.vector.quantize_mx(
                out=tcod[pr][:].bitcast(FP8X4), scales=tscl[pr][:], in_=tb[pr // 2][:, pr % 2].rearrange("p g n t -> p (g n t)")
            )

        def interleave_blocks(copy, pr, b0, b1, m0, n0, n):
            copy(
                out=wb[pr][:, m0 + b0 * n : m0 + b1 * n, :].rearrange("p (b c i) j -> p b c j i", b=b1 - b0, i=RUN),
                in_=wr[pr][:, b0:b1, :, n0 : n0 + n].rearrange("p b j (c i) -> p b c j i", i=RUN),
            )

        def interleave_weights(pr, half=0):
            if half == 0:
                wb[pr] = stage.tile([P, 4 * N, 4], BF16, name="wb", tag="wb", bufs=WB_BUFS, align_bytes=64)
            m0, n0, n = (half * 2 * N, half * P, P) if pr in HS else (0, 0, N)
            nv = VBLOCKS[pr] if half == 0 else 0
            ns = 4 - nv
            if ns:
                interleave_blocks(nc.gpsimd.tensor_copy if pr in GP else nc.scalar.copy, pr, 0, ns, m0, n0, n)
            if nv % 2:
                interleave_blocks(nc.vector.tensor_copy, pr, ns, ns + 1, m0, n0, n)
            if nv >= 2:
                interleave_blocks(nc.vector.tensor_copy, pr, ns + nv % 2, 4, m0, n0, n)

        def quantize_weights(pr, half=0):
            if half == 0:
                wcod[pr] = stage.tile([P, 4 * N], U32, name="wcod", tag="wcod", bufs=WQ_BUFS, align_bytes=64)
                wscl[pr] = stage.tile([P, 4 * N], U8, name="wscl", tag="wscl", bufs=WQ_BUFS, align_bytes=64)
            cols = slice(half * 2 * N, (half + 1) * 2 * N) if pr in HS else slice(0, 4 * N)
            nc.vector.quantize_mx(
                out=wcod[pr][:, cols].bitcast(FP8X4), scales=wscl[pr][:, cols], in_=wb[pr][:, cols, :].rearrange("p m j -> p (m j)")
            )

        def multiply(pr, halves=(0, 1)):
            for h in halves:
                for i in range(2):
                    e = 2 * pr + i
                    c, s0 = e // 4, (e % 4) * C
                    for g in range(2):
                        w0 = ((2 * h + i) * 2 + g) * P if pr in HS else (2 * i + g) * N + h * P
                        nc.tensor.matmul_mx(
                            out=acc[h][c][:, s0 : s0 + C],
                            lhsT=wcod[pr][:, w0 : w0 + P].bitcast(FP8X4),
                            lhsT_scale=wscl[pr][:, w0 : w0 + P],
                            rhs=tcod[pr][:, (2 * g + i) * C : (2 * g + i + 1) * C].bitcast(FP8X4),
                            rhs_scale=tscl[pr][:, (2 * g + i) * C : (2 * g + i + 1) * C],
                            start=(g == 0),
                            stop=(g == 1),
                        )

        def empty(h, q):
            nc.scalar.copy(out=y[h][:, q * 4 * C : (q + 1) * 4 * C], in_=acc[h][q][:])

        for t in range(4):
            nc.scalar.copy(out=xb[:, t, :], in_=x1[:, t, :])
        with tc.tile_pool(name="gst", bufs=1) as gst:
            for c in range(4):
                gather0(gst, c)
            for op in STOK:
                if op[0] == "F":
                    gather1(op[1], op[2], op[3])
                else:
                    interleave0(op[1])
            for pr in range(2):
                quantize_tokens(pr)
            for pr in range(2):
                interleave_weights(pr)
            for pr in range(PAIRS):
                quantize_weights(pr)
                multiply(pr, (0,) if pr in HS else (0, 1))
                if pr + 2 < PAIRS:
                    interleave_weights(pr + 2)
                    quantize_tokens(pr + 2)
            for q in range(E // 4):
                empty(0, q)
            for pr in HS:
                interleave_weights(pr, 1)
            for pr in HS:
                quantize_weights(pr, 1)
                multiply(pr, (1,))
        late = [stage.tile([P, E * C], F32, name="late%d" % k, tag="wb", bufs=WB_BUFS, align_bytes=64) for k in range(3)]
        y.append(late[2])
        for q in range(E // 4):
            empty(1, q)

        fin = ctx.enter_context(tc.tile_pool(name="fin", bufs=2))
        steps = []
        for h in range(2):
            t0 = 0
            for n in TOKS[h]:
                steps.append((h, t0, n))
                t0 += n
        parts = {}

        def fetch(s):
            h, t0, n = steps[s]
            for r in range(2):
                parts[s, r] = late[r][:, 0:n] if s == 0 else fin.tile([P, n], F32, name="part%d" % r, tag="part%d" % r)[:]
                nc.vector.tensor_tensor(
                    parts[s, r],
                    y[h][:].indirect(pos_sb[r][:] if n == T else pos_sb[r][:, t0 // 16 : (t0 + n) // 16]),
                    gt[:, h, r, t0 : t0 + n],
                    MULT,
                )

        def finish(s):
            h, t0, n = steps[s]
            o = fin.tile([P, n], F32, name="o", tag="o", bufs=3)
            if s < PE_ADDS:
                blocks = range(n // 512)
                banks = [psum.tile([P, 512], F32, name="sum%d" % k, tag="acc0_%d" % k) for k in blocks]
                for r in range(2):
                    for k in blocks:
                        nc.tensor.matmul(banks[k][:], ident[:], parts[s, r][:, k * 512 : (k + 1) * 512], start=(r == 0), stop=(r == 1))
                for k in blocks:
                    nc.scalar.copy(out=o[:, k * 512 : (k + 1) * 512], in_=banks[k][:])
                    nc.scalar.dma_start(out=out[h * P : (h + 1) * P, t0 + k * 512 : t0 + (k + 1) * 512], in_=o[:, k * 512 : (k + 1) * 512])
            else:
                nc.vector.tensor_tensor(o[:], parts[s, 0], parts[s, 1], ADD)
                nc.sync.dma_start(out=out[h * P : (h + 1) * P, t0 : t0 + n], in_=o[:])

        fetch(0)
        for s in range(1, len(steps)):
            fetch(s)
            finish(s - 1)
        finish(len(steps) - 1)
